import numpy as np
import ml_dtypes


def mxq(x, axis, fmt="e4m3"):
    dtype, down = {"e4m3": (ml_dtypes.float8_e4m3fn, 7), "e5m2": (ml_dtypes.float8_e5m2, 14)}[fmt]
    v = np.moveaxis(np.asarray(x, np.float32).astype(ml_dtypes.bfloat16).astype(np.float64), axis, -1)
    blocks = v.reshape(v.shape[:-1] + (-1, 32))
    amax = np.abs(blocks).max(-1, keepdims=True)
    byte = np.maximum(np.where(amax > 0, np.frexp(amax)[1] - 1 + 127, 0) - down, 1)
    scale = np.exp2(byte - 127.0)
    codes = (blocks / scale).astype(np.float32).astype(dtype).astype(np.float64)
    return np.moveaxis((codes * scale).reshape(v.shape), -1, axis)


WIDE = False


def mx_kscale(k):
    if not WIDE:
        return np.ones(k)
    levels = np.array([10, -10, 5, -5, 0])
    if k % 512:
        return np.exp2(np.random.permutation(np.resize(levels, k // 32))).repeat(32)
    a = np.empty((k // 512, 16))
    for p in range(k // 512):
        a[p, :8] = np.random.permutation(np.resize(levels, 8))
        for g in range(8):
            far = levels[np.abs(levels - a[p, g]) >= 10]
            a[p, g + 8] = far[np.random.randint(len(far))]
    return np.exp2(a.ravel()).repeat(32)


def f64(x):
    return np.asarray(x).astype(np.float64)


def striped(idx):
    return np.tile(idx.reshape(-1, 16).T, (8, 1)).astype(np.uint16)


def unstriped(offs):
    return offs[:16].T.reshape(-1).astype(np.int64)


def pack_weight(w):
    k, n = w.shape
    w = f64(np.asarray(w, np.float32).astype(ml_dtypes.bfloat16)).reshape(k // 32, 32, n)
    amax = np.abs(w).max(1)
    byte = np.clip(np.where(amax > 0, np.frexp(amax)[1] - 1 + 127 - 7, 1), 1, 254)
    scaled = (w * np.exp2(127.0 - byte)[:, None, :]).reshape(k, n).astype(np.float32)
    words = np.ascontiguousarray(scaled.reshape(k // 512, 128, 4, n).transpose(0, 1, 3, 2)).astype(ml_dtypes.float8_e4m3fn).view(np.uint8)
    return words, np.ascontiguousarray(byte.astype(np.uint8).reshape(k // 512, 16, n))


def unpack_weight(words, scales):
    g, p, n, _ = words.shape
    vals = np.ascontiguousarray(words).view(ml_dtypes.float8_e4m3fn).astype(np.float64) * np.repeat(np.exp2(scales.astype(np.float64) - 127.0), 8, axis=1)[..., None]
    return vals.transpose(0, 1, 3, 2).reshape(g * 512, n)


K, T, S, N = 1024, 2048, 512, 128


def setup_inputs():
    n = np.random.standard_normal
    s = mx_kscale(K)[:, None]
    packed_w1 = pack_weight(n((K, N)) / np.sqrt(K) / s)
    packed_w2 = pack_weight(n((K, N)) / np.sqrt(K) / s)
    packed_w3 = pack_weight(n((K, N)) / np.sqrt(K) / s)
    return {
        "xT": (n((K, T)) * s).astype(np.float32),
        "w1_words": packed_w1[0],
        "w1_scales": packed_w1[1],
        "w2_words": packed_w2[0],
        "w2_scales": packed_w2[1],
        "w3_words": packed_w3[0],
        "w3_scales": packed_w3[1],
        "offs": striped(np.random.permutation(T)[:S]),
    }


def reference(xT, w1_words, w1_scales, w2_words, w2_scales, w3_words, w3_scales, offs):
    xq = mxq(f64(xT)[:, unstriped(offs)], 0, "e4m3")
    return np.minimum(np.minimum(unpack_weight(w1_words, w1_scales).T @ xq, unpack_weight(w2_words, w2_scales).T @ xq), unpack_weight(w3_words, w3_scales).T @ xq)

@@ -1,0 +1,128 @@
+from contextlib import ExitStack
+
+import concourse.mybir as mybir
+
+K, T, S, N = 1024, 2048, 512, 128
+FLOPS = 3 * 2 * K * S * N
+
+F32 = mybir.dt.float32
+BF16 = mybir.dt.bfloat16
+I32 = mybir.dt.int32
+U32 = mybir.dt.uint32
+U16 = mybir.dt.uint16
+U8 = mybir.dt.uint8
+FP8X4 = mybir.dt.float8_e4m3fn_x4
+MIN = mybir.AluOpType.min
+
+P = 128
+PACK = 4
+PASSES = K // (P * PACK)
+HALF = S // 2
+LIST_COLS = HALF // 16
+
+
+def tile_picked_maxout_min_e_kernel(
+    tc, xT, w1_words, w1_scales, w2_words, w2_scales, w3_words, w3_scales, offs, out
+):
+    nc = tc.nc
+    w_words = (w1_words, w2_words, w3_words)
+    w_scales = (w1_scales, w2_scales, w3_scales)
+    x_rows = xT.rearrange("(z p j) t -> z p j t", z=PASSES, j=PACK)
+
+    with ExitStack() as ctx:
+        keep = ctx.enter_context(tc.tile_pool(name="keep", bufs=1))
+        psum = ctx.enter_context(tc.psum_pool(name="psum", bufs=1))
+
+        offsets = keep.tile([P, S // 16], U16, name="offsets")
+        nc.sync.dma_start(offsets[:], offs)
+
+        scale_tiles = []
+        for m in range(3):
+            st = keep.tile([P, PASSES, N], U8, name="wscale%d" % m, align_bytes=64)
+            nc.gpsimd.memset(st[:].rearrange("p z n -> p (z n)").bitcast(I32), 0)
+            scale_tiles.append(st)
+        for m in range(3):
+            for q in range(4):
+                nc.gpsimd.dma_start(
+                    out=scale_tiles[m][32 * q : 32 * q + 4, :, :].bitcast(I32),
+                    in_=w_scales[m][:, 4 * q : 4 * q + 4, :].rearrange("z r n -> r z n").bitcast(I32),
+                )
+
+        picked0 = keep.tile([P, PACK, S], F32, name="picked0")
+        for u in range(2):
+            pair = keep.tile([P, 2, T], F32, name="xpair%d" % u)
+            nc.sync.dma_start(out=pair[:], in_=x_rows[0, :, 2 * u : 2 * u + 2, :])
+            for e in range(2):
+                nc.vector.tensor_copy(picked0[:, 2 * u + e, :], pair[:, e, :].indirect(offsets[:]))
+        grouped0 = keep.tile([P, S, PACK], BF16, name="grouped0", align_bytes=64)
+        nc.scalar.copy(out=grouped0[:], in_=picked0[:].rearrange("p j s -> p s j"))
+        codes0 = keep.tile([P, S], U32, name="codes0", align_bytes=64)
+        scales0 = keep.tile([P, S], U8, name="scales0", align_bytes=64)
+        nc.vector.quantize_mx(
+            out=codes0[:].bitcast(FP8X4), scales=scales0[:], in_=grouped0[:].rearrange("p s j -> p (s j)")
+        )
+
+        grouped1 = [keep.tile([P, HALF, PACK], BF16, name="grouped1_%d" % h, align_bytes=64) for h in range(2)]
+        for j in range(PACK):
+            plane = keep.tile([P, T], F32, name="xplane%d" % j)
+            nc.sync.dma_start(out=plane[:], in_=x_rows[1, :, j, :])
+            for h in range(2):
+                nc.vector.tensor_copy(
+                    grouped1[h][:, :, j], plane[:].indirect(offsets[:, h * LIST_COLS : (h + 1) * LIST_COLS])
+                )
+
+        words = {}
+        for z in range(PASSES):
+            for m in range(3):
+                wt = keep.tile([P, N], U32, name="wwords%d_%d" % (z, m), align_bytes=64)
+                nc.sync.dma_start(
+                    out=wt[:].bitcast(I32), in_=w_words[m][z].rearrange("p n t -> p (n t)").bitcast(I32)
+                )
+                words[(z, m)] = wt
+
+        banks = {}
+        for m in range(3):
+            for h in range(2):
+                bank = psum.tile([N, HALF], F32, name="bank%d_%d" % (m, h))
+                banks[(m, h)] = bank
+                cols = slice(h * HALF, (h + 1) * HALF)
+                nc.tensor.matmul_mx(
+                    out=bank[:],
+                    lhsT=words[(0, m)][:].bitcast(FP8X4),
+                    lhsT_scale=scale_tiles[m][:, 0, :],
+                    rhs=codes0[:, cols].bitcast(FP8X4),
+                    rhs_scale=scales0[:, cols],
+                    start=True,
+                    stop=False,
+                )
+
+        codes1 = []
+        scales1 = []
+        for h in range(2):
+            c1 = keep.tile([P, HALF], U32, name="codes1_%d" % h, align_bytes=64)
+            s1 = keep.tile([P, HALF], U8, name="scales1_%d" % h, align_bytes=64)
+            nc.vector.quantize_mx(
+                out=c1[:].bitcast(FP8X4), scales=s1[:], in_=grouped1[h][:].rearrange("p s j -> p (s j)")
+            )
+            codes1.append(c1)
+            scales1.append(s1)
+        for h in range(2):
+            for m in range(3):
+                nc.tensor.matmul_mx(
+                    out=banks[(m, h)][:],
+                    lhsT=words[(1, m)][:].bitcast(FP8X4),
+                    lhsT_scale=scale_tiles[m][:, 1, :],
+                    rhs=codes1[h][:].bitcast(FP8X4),
+                    rhs_scale=scales1[h][:],
+                    start=False,
+                    stop=True,
+                )
+
+        for h in range(2):
+            first = keep.tile([N, HALF], F32, name="first%d" % h)
+            nc.scalar.copy(out=first[:], in_=banks[(0, h)][:])
+            two = keep.tile([N, HALF], F32, name="two%d" % h)
+            nc.vector.tensor_tensor(two[:], banks[(1, h)][:], first[:], MIN)
+            three = keep.tile([N, HALF], F32, name="three%d" % h)
+            nc.vector.tensor_tensor(three[:], banks[(2, h)][:], two[:], MIN)
+            nc.sync.dma_start(out=out[:, h * HALF : (h + 1) * HALF], in_=three[:])

@@ -33,44 +33,15 @@ def tile_picked_maxout_min_e_kernel(
         keep = ctx.enter_context(tc.tile_pool(name="keep", bufs=1))
         psum = ctx.enter_context(tc.psum_pool(name="psum", bufs=1))
 
+        pairs = [keep.tile([P, 2, T], F32, name="xpair%d" % u) for u in range(3)]
+        planes = [keep.tile([P, T], F32, name="xplane%d" % j) for j in range(2)]
         offsets = keep.tile([P, S // 16], U16, name="offsets")
+        nc.sync.dma_start(out=pairs[0][:], in_=x_rows[0, :, 0:2, :])
         nc.sync.dma_start(offsets[:], offs)
-
-        scale_tiles = []
-        for m in range(3):
-            st = keep.tile([P, PASSES, N], U8, name="wscale%d" % m, align_bytes=64)
-            nc.gpsimd.memset(st[:].rearrange("p z n -> p (z n)").bitcast(I32), 0)
-            scale_tiles.append(st)
-        for m in range(3):
-            for q in range(4):
-                nc.gpsimd.dma_start(
-                    out=scale_tiles[m][32 * q : 32 * q + 4, :, :].bitcast(I32),
-                    in_=w_scales[m][:, 4 * q : 4 * q + 4, :].rearrange("z r n -> r z n").bitcast(I32),
-                )
-
-        picked0 = keep.tile([P, PACK, S], F32, name="picked0")
-        for u in range(2):
-            pair = keep.tile([P, 2, T], F32, name="xpair%d" % u)
-            nc.sync.dma_start(out=pair[:], in_=x_rows[0, :, 2 * u : 2 * u + 2, :])
-            for e in range(2):
-                nc.vector.tensor_copy(picked0[:, 2 * u + e, :], pair[:, e, :].indirect(offsets[:]))
-        grouped0 = keep.tile([P, S, PACK], BF16, name="grouped0", align_bytes=64)
-        nc.scalar.copy(out=grouped0[:], in_=picked0[:].rearrange("p j s -> p s j"))
-        codes0 = keep.tile([P, S], U32, name="codes0", align_bytes=64)
-        scales0 = keep.tile([P, S], U8, name="scales0", align_bytes=64)
-        nc.vector.quantize_mx(
-            out=codes0[:].bitcast(FP8X4), scales=scales0[:], in_=grouped0[:].rearrange("p s j -> p (s j)")
-        )
-
-        grouped1 = [keep.tile([P, HALF, PACK], BF16, name="grouped1_%d" % h, align_bytes=64) for h in range(2)]
-        for j in range(PACK):
-            plane = keep.tile([P, T], F32, name="xplane%d" % j)
-            nc.sync.dma_start(out=plane[:], in_=x_rows[1, :, j, :])
-            for h in range(2):
-                nc.vector.tensor_copy(
-                    grouped1[h][:, :, j], plane[:].indirect(offsets[:, h * LIST_COLS : (h + 1) * LIST_COLS])
-                )
-
+        nc.sync.dma_start(out=pairs[1][:], in_=x_rows[0, :, 2:4, :])
+        nc.sync.dma_start(out=pairs[2][:], in_=x_rows[1, :, 0:2, :])
+        for j in range(2):
+            nc.sync.dma_start(out=planes[j][:], in_=x_rows[1, :, 2 + j, :])
         words = {}
         for z in range(PASSES):
             for m in range(3):
@@ -79,6 +50,50 @@ def tile_picked_maxout_min_e_kernel(
                     out=wt[:].bitcast(I32), in_=w_words[m][z].rearrange("p n t -> p (n t)").bitcast(I32)
                 )
                 words[(z, m)] = wt
+
+        wscale = keep.tile([P, 3 * PASSES * N], U8, name="wscale", align_bytes=64)
+        nc.gpsimd.memset(wscale[:].bitcast(I32), 0)
+        for m in range(3):
+            nc.gpsimd.dma_start(
+                out=wscale[0:16, m * PASSES * N : (m + 1) * PASSES * N].rearrange("r (z n) -> r z n", z=PASSES).bitcast(I32),
+                in_=w_scales[m].rearrange("z r n -> r z n").bitcast(I32),
+            )
+        for q in range(1, 4):
+            nc.gpsimd.dma_start(
+                out=wscale[32 * q : 32 * q + 4, :].bitcast(I32), in_=wscale[4 * q : 4 * q + 4, :].bitcast(I32)
+            )
+
+        def half_list(h):
+            return offsets[:, h * LIST_COLS : (h + 1) * LIST_COLS]
+
+        grouped0 = keep.tile([P, S, PACK], BF16, name="grouped0", align_bytes=64)
+        for e in range(2):
+            nc.vector.tensor_copy(grouped0[:, :, e], pairs[0][:, e, :].indirect(offsets[:]))
+        picked0 = keep.tile([P, 2, S], F32, name="picked0")
+        for e in range(2):
+            nc.vector.tensor_copy(picked0[:, e, :], pairs[1][:, e, :].indirect(offsets[:]))
+        nc.scalar.copy(out=grouped0[:, :, 2:4], in_=picked0[:].rearrange("p j s -> p s j"))
+
+        grouped1 = [keep.tile([P, HALF, PACK], BF16, name="grouped1_%d" % h, align_bytes=64) for h in range(2)]
+        picked1 = keep.tile([P, 2, S], F32, name="picked1")
+        codes0 = keep.tile([P, S], U32, name="codes0", align_bytes=64)
+        scales0 = keep.tile([P, S], U8, name="scales0", align_bytes=64)
+        nc.vector.quantize_mx(
+            out=codes0[:].bitcast(FP8X4), scales=scales0[:], in_=grouped0[:].rearrange("p s j -> p (s j)")
+        )
+        for e in range(2):
+            nc.vector.tensor_copy(picked1[:, e, :], pairs[2][:, e, :].indirect(offsets[:]))
+        for h in range(2):
+            nc.scalar.copy(
+                out=grouped1[h][:, :, 0:2], in_=picked1[:, :, h * HALF : (h + 1) * HALF].rearrange("p j s -> p s j")
+            )
+        for j in range(2):
+            for h in range(2):
+                nc.vector.tensor_copy(grouped1[h][:, :, 2 + j], planes[j][:].indirect(half_list(h)))
+
+        def w_scale(z, m):
+            first = (m * PASSES + z) * N
+            return wscale[:, first : first + N]
 
         banks = {}
         for m in range(3):
@@ -89,7 +104,7 @@ def tile_picked_maxout_min_e_kernel(
                 nc.tensor.matmul_mx(
                     out=bank[:],
                     lhsT=words[(0, m)][:].bitcast(FP8X4),
-                    lhsT_scale=scale_tiles[m][:, 0, :],
+                    lhsT_scale=w_scale(0, m),
                     rhs=codes0[:, cols].bitcast(FP8X4),
                     rhs_scale=scales0[:, cols],
                     start=True,
@@ -111,7 +126,7 @@ def tile_picked_maxout_min_e_kernel(
                 nc.tensor.matmul_mx(
                     out=banks[(m, h)][:],
                     lhsT=words[(1, m)][:].bitcast(FP8X4),
-                    lhsT_scale=scale_tiles[m][:, 1, :],
+                    lhsT_scale=w_scale(1, m),
                     rhs=codes1[h][:].bitcast(FP8X4),
                     rhs_scale=scales1[h][:],
                     start=False,

@@ -38,10 +38,21 @@ def tile_picked_maxout_min_e_kernel(
         offsets = keep.tile([P, S // 16], U16, name="offsets")
         nc.sync.dma_start(out=pairs[0][:], in_=x_rows[0, :, 0:2, :])
         nc.sync.dma_start(offsets[:], offs)
+        wscale = keep.tile([P, 3 * PASSES * N], U8, name="wscale", align_bytes=64)
+        nc.vector.memset(wscale[:].bitcast(I32), 0)
+        for m in range(3):
+            nc.sync.dma_start(
+                out=wscale[0:16, m * PASSES * N : (m + 1) * PASSES * N].rearrange("r (z n) -> r z n", z=PASSES).bitcast(I32),
+                in_=w_scales[m].rearrange("z r n -> r z n").bitcast(I32),
+            )
         nc.sync.dma_start(out=pairs[1][:], in_=x_rows[0, :, 2:4, :])
         nc.sync.dma_start(out=pairs[2][:], in_=x_rows[1, :, 0:2, :])
         for j in range(2):
             nc.sync.dma_start(out=planes[j][:], in_=x_rows[1, :, 2 + j, :])
+        for q in range(1, 4):
+            nc.sync.dma_start(
+                out=wscale[32 * q : 32 * q + 4, :].bitcast(I32), in_=wscale[4 * q : 4 * q + 4, :].bitcast(I32)
+            )
         words = {}
         for z in range(PASSES):
             for m in range(3):
@@ -49,19 +60,7 @@ def tile_picked_maxout_min_e_kernel(
                 nc.sync.dma_start(
                     out=wt[:].bitcast(I32), in_=w_words[m][z].rearrange("p n t -> p (n t)").bitcast(I32)
                 )
-                words[(z, m)] = wt
-
-        wscale = keep.tile([P, 3 * PASSES * N], U8, name="wscale", align_bytes=64)
-        nc.gpsimd.memset(wscale[:].bitcast(I32), 0)
-        for m in range(3):
-            nc.gpsimd.dma_start(
-                out=wscale[0:16, m * PASSES * N : (m + 1) * PASSES * N].rearrange("r (z n) -> r z n", z=PASSES).bitcast(I32),
-                in_=w_scales[m].rearrange("z r n -> r z n").bitcast(I32),
-            )
-        for q in range(1, 4):
-            nc.gpsimd.dma_start(
-                out=wscale[32 * q : 32 * q + 4, :].bitcast(I32), in_=wscale[4 * q : 4 * q + 4, :].bitcast(I32)
-            )
+                words[(z, m)] = wt[:]
 
         def half_list(h):
             return offsets[:, h * LIST_COLS : (h + 1) * LIST_COLS]
@@ -103,7 +102,7 @@ def tile_picked_maxout_min_e_kernel(
                 cols = slice(h * HALF, (h + 1) * HALF)
                 nc.tensor.matmul_mx(
                     out=bank[:],
-                    lhsT=words[(0, m)][:].bitcast(FP8X4),
+                    lhsT=words[(0, m)].bitcast(FP8X4),
                     lhsT_scale=w_scale(0, m),
                     rhs=codes0[:, cols].bitcast(FP8X4),
                     rhs_scale=scales0[:, cols],
@@ -121,11 +120,11 @@ def tile_picked_maxout_min_e_kernel(
             )
             codes1.append(c1)
             scales1.append(s1)
-        for h in range(2):
-            for m in range(3):
+        for m in range(3):
+            for h in range(2):
                 nc.tensor.matmul_mx(
                     out=banks[(m, h)][:],
-                    lhsT=words[(1, m)][:].bitcast(FP8X4),
+                    lhsT=words[(1, m)].bitcast(FP8X4),
                     lhsT_scale=w_scale(1, m),
                     rhs=codes1[h][:].bitcast(FP8X4),
                     rhs_scale=scales1[h][:],
@@ -133,11 +132,15 @@ def tile_picked_maxout_min_e_kernel(
                     stop=True,
                 )
 
+        lowest = []
         for h in range(2):
             first = keep.tile([N, HALF], F32, name="first%d" % h)
             nc.scalar.copy(out=first[:], in_=banks[(0, h)][:])
-            two = keep.tile([N, HALF], F32, name="two%d" % h)
-            nc.vector.tensor_tensor(two[:], banks[(1, h)][:], first[:], MIN)
-            three = keep.tile([N, HALF], F32, name="three%d" % h)
-            nc.vector.tensor_tensor(three[:], banks[(2, h)][:], two[:], MIN)
-            nc.sync.dma_start(out=out[:, h * HALF : (h + 1) * HALF], in_=three[:])
+            lowest.append(first)
+        for m in range(1, 3):
+            for h in range(2):
+                lower = keep.tile([N, HALF], F32, name="lower%d_%d" % (m, h))
+                nc.vector.tensor_tensor(lower[:], banks[(m, h)][:], lowest[h][:], MIN)
+                lowest[h] = lower
+        for h in range(2):
+            nc.sync.dma_start(out=out[:, h * HALF : (h + 1) * HALF], in_=lowest[h][:])

@@ -66,12 +66,8 @@ def tile_picked_maxout_min_e_kernel(
             return offsets[:, h * LIST_COLS : (h + 1) * LIST_COLS]
 
         grouped0 = keep.tile([P, S, PACK], BF16, name="grouped0", align_bytes=64)
-        for e in range(2):
-            nc.vector.tensor_copy(grouped0[:, :, e], pairs[0][:, e, :].indirect(offsets[:]))
-        picked0 = keep.tile([P, 2, S], F32, name="picked0")
-        for e in range(2):
-            nc.vector.tensor_copy(picked0[:, e, :], pairs[1][:, e, :].indirect(offsets[:]))
-        nc.scalar.copy(out=grouped0[:, :, 2:4], in_=picked0[:].rearrange("p j s -> p s j"))
+        for j in range(PACK):
+            nc.vector.tensor_copy(grouped0[:, :, j], pairs[j // 2][:, j % 2, :].indirect(offsets[:]))
 
         grouped1 = [keep.tile([P, HALF, PACK], BF16, name="grouped1_%d" % h, align_bytes=64) for h in range(2)]
         picked1 = keep.tile([P, 2, S], F32, name="picked1")

@@ -38,21 +38,10 @@ def tile_picked_maxout_min_e_kernel(
         offsets = keep.tile([P, S // 16], U16, name="offsets")
         nc.sync.dma_start(out=pairs[0][:], in_=x_rows[0, :, 0:2, :])
         nc.sync.dma_start(offsets[:], offs)
-        wscale = keep.tile([P, 3 * PASSES * N], U8, name="wscale", align_bytes=64)
-        nc.vector.memset(wscale[:].bitcast(I32), 0)
-        for m in range(3):
-            nc.sync.dma_start(
-                out=wscale[0:16, m * PASSES * N : (m + 1) * PASSES * N].rearrange("r (z n) -> r z n", z=PASSES).bitcast(I32),
-                in_=w_scales[m].rearrange("z r n -> r z n").bitcast(I32),
-            )
         nc.sync.dma_start(out=pairs[1][:], in_=x_rows[0, :, 2:4, :])
         nc.sync.dma_start(out=pairs[2][:], in_=x_rows[1, :, 0:2, :])
         for j in range(2):
             nc.sync.dma_start(out=planes[j][:], in_=x_rows[1, :, 2 + j, :])
-        for q in range(1, 4):
-            nc.sync.dma_start(
-                out=wscale[32 * q : 32 * q + 4, :].bitcast(I32), in_=wscale[4 * q : 4 * q + 4, :].bitcast(I32)
-            )
         words = {}
         for z in range(PASSES):
             for m in range(3):
@@ -60,7 +49,19 @@ def tile_picked_maxout_min_e_kernel(
                 nc.sync.dma_start(
                     out=wt[:].bitcast(I32), in_=w_words[m][z].rearrange("p n t -> p (n t)").bitcast(I32)
                 )
-                words[(z, m)] = wt[:]
+                words[(z, m)] = wt
+
+        wscale = keep.tile([P, 3 * PASSES * N], U8, name="wscale", align_bytes=64)
+        nc.gpsimd.memset(wscale[:].bitcast(I32), 0)
+        for m in range(3):
+            nc.gpsimd.dma_start(
+                out=wscale[0:16, m * PASSES * N : (m + 1) * PASSES * N].rearrange("r (z n) -> r z n", z=PASSES).bitcast(I32),
+                in_=w_scales[m].rearrange("z r n -> r z n").bitcast(I32),
+            )
+        for q in range(1, 4):
+            nc.gpsimd.dma_start(
+                out=wscale[32 * q : 32 * q + 4, :].bitcast(I32), in_=wscale[4 * q : 4 * q + 4, :].bitcast(I32)
+            )
 
         def half_list(h):
             return offsets[:, h * LIST_COLS : (h + 1) * LIST_COLS]
@@ -98,7 +99,7 @@ def tile_picked_maxout_min_e_kernel(
                 cols = slice(h * HALF, (h + 1) * HALF)
                 nc.tensor.matmul_mx(
                     out=bank[:],
-                    lhsT=words[(0, m)].bitcast(FP8X4),
+                    lhsT=words[(0, m)][:].bitcast(FP8X4),
                     lhsT_scale=w_scale(0, m),
                     rhs=codes0[:, cols].bitcast(FP8X4),
                     rhs_scale=scales0[:, cols],
@@ -120,7 +121,7 @@ def tile_picked_maxout_min_e_kernel(
             for h in range(2):
                 nc.tensor.matmul_mx(
                     out=banks[(m, h)][:],
-                    lhsT=words[(1, m)].bitcast(FP8X4),
+                    lhsT=words[(1, m)][:].bitcast(FP8X4),
                     lhsT_scale=w_scale(1, m),
                     rhs=codes1[h][:].bitcast(FP8X4),
                     rhs_scale=scales1[h][:],

@@ -18,6 +18,7 @@ P = 128
 PACK = 4
 PASSES = K // (P * PACK)
 HALF = S // 2
+QUARTER = S // 4
 LIST_COLS = HALF // 16
 
 
@@ -42,26 +43,26 @@ def tile_picked_maxout_min_e_kernel(
         nc.sync.dma_start(out=pairs[2][:], in_=x_rows[1, :, 0:2, :])
         for j in range(2):
             nc.sync.dma_start(out=planes[j][:], in_=x_rows[1, :, 2 + j, :])
-        words = {}
-        for z in range(PASSES):
-            for m in range(3):
-                wt = keep.tile([P, N], U32, name="wwords%d_%d" % (z, m), align_bytes=64)
-                nc.sync.dma_start(
-                    out=wt[:].bitcast(I32), in_=w_words[m][z].rearrange("p n t -> p (n t)").bitcast(I32)
-                )
-                words[(z, m)] = wt
-
-        wscale = keep.tile([P, 3 * PASSES * N], U8, name="wscale", align_bytes=64)
+        wscale = keep.tile([P, PASSES, 3 * N], U8, name="wscale", align_bytes=64)
         nc.gpsimd.memset(wscale[:].bitcast(I32), 0)
         for m in range(3):
             nc.gpsimd.dma_start(
-                out=wscale[0:16, m * PASSES * N : (m + 1) * PASSES * N].rearrange("r (z n) -> r z n", z=PASSES).bitcast(I32),
+                out=wscale[0:16, :, m * N : (m + 1) * N].bitcast(I32),
                 in_=w_scales[m].rearrange("z r n -> r z n").bitcast(I32),
             )
         for q in range(1, 4):
+            moved = slice(0, PASSES if q < 3 else 1)
             nc.gpsimd.dma_start(
-                out=wscale[32 * q : 32 * q + 4, :].bitcast(I32), in_=wscale[4 * q : 4 * q + 4, :].bitcast(I32)
+                out=wscale[32 * q : 32 * q + 4, moved, :].bitcast(I32), in_=wscale[4 * q : 4 * q + 4, moved, :].bitcast(I32)
             )
+
+        words = {}
+        for z, m in ((0, 0), (0, 1), (1, 0), (1, 1), (0, 2), (1, 2)):
+            wt = keep.tile([P, N], U32, name="wwords%d_%d" % (z, m), align_bytes=64)
+            nc.sync.dma_start(out=wt[:].bitcast(I32), in_=w_words[m][z].rearrange("p n t -> p (n t)").bitcast(I32))
+            words[(z, m)] = wt
+            if (z, m) == (1, 1):
+                nc.sync.dma_start(out=wscale[96:100, 1, :].bitcast(I32), in_=wscale[12:16, 1, :].bitcast(I32))
 
         def half_list(h):
             return offsets[:, h * LIST_COLS : (h + 1) * LIST_COLS]
@@ -88,56 +89,60 @@ def tile_picked_maxout_min_e_kernel(
                 nc.vector.tensor_copy(grouped1[h][:, :, 2 + j], planes[j][:].indirect(half_list(h)))
 
         def w_scale(z, m):
-            first = (m * PASSES + z) * N
-            return wscale[:, first : first + N]
+            return wscale[:, z, m * N : (m + 1) * N]
 
-        banks = {}
-        for m in range(3):
-            for h in range(2):
-                bank = psum.tile([N, HALF], F32, name="bank%d_%d" % (m, h))
-                banks[(m, h)] = bank
-                cols = slice(h * HALF, (h + 1) * HALF)
-                nc.tensor.matmul_mx(
-                    out=bank[:],
-                    lhsT=words[(0, m)][:].bitcast(FP8X4),
-                    lhsT_scale=w_scale(0, m),
-                    rhs=codes0[:, cols].bitcast(FP8X4),
-                    rhs_scale=scales0[:, cols],
-                    start=True,
-                    stop=False,
-                )
-
-        codes1 = []
-        scales1 = []
-        for h in range(2):
-            c1 = keep.tile([P, HALF], U32, name="codes1_%d" % h, align_bytes=64)
-            s1 = keep.tile([P, HALF], U8, name="scales1_%d" % h, align_bytes=64)
+        codes1 = keep.tile([P, S], U32, name="codes1", align_bytes=64)
+        scales1 = keep.tile([P, S], U8, name="scales1", align_bytes=64)
+        for h, first, width in [(h, q * QUARTER, QUARTER) for h in range(2) for q in range(2)]:
+            cols = slice(h * HALF + first, h * HALF + first + width)
             nc.vector.quantize_mx(
-                out=c1[:].bitcast(FP8X4), scales=s1[:], in_=grouped1[h][:].rearrange("p s j -> p (s j)")
+                out=codes1[:, cols].bitcast(FP8X4),
+                scales=scales1[:, cols],
+                in_=grouped1[h][:, first : first + width, :].rearrange("p s j -> p (s j)"),
             )
-            codes1.append(c1)
-            scales1.append(s1)
-        for m in range(3):
-            for h in range(2):
-                nc.tensor.matmul_mx(
-                    out=banks[(m, h)][:],
-                    lhsT=words[(1, m)][:].bitcast(FP8X4),
-                    lhsT_scale=w_scale(1, m),
-                    rhs=codes1[h][:].bitcast(FP8X4),
-                    rhs_scale=scales1[h][:],
-                    start=False,
-                    stop=True,
-                )
 
-        lowest = []
+        codes = (codes0, codes1)
+        scales = (scales0, scales1)
+        pieces = [(0, q * QUARTER, QUARTER) for q in range(4)] + [(m, h * HALF, HALF) for m in (1, 2) for h in range(2)]
+        banks = {(m, first): psum.tile([N, width], F32, name="bank%d_%d" % (m, first)) for m, first, width in pieces}
+
+        def one_pass(z, m, first, width):
+            cols = slice(first, first + width)
+            nc.tensor.matmul_mx(
+                out=banks[(m, first)][:],
+                lhsT=words[(z, m)][:].bitcast(FP8X4),
+                lhsT_scale=w_scale(z, m),
+                rhs=codes[z][:, cols].bitcast(FP8X4),
+                rhs_scale=scales[z][:, cols],
+                start=z == 0,
+                stop=z == PASSES - 1,
+            )
+
+        for m, first, width in pieces[:6]:
+            one_pass(0, m, first, width)
         for h in range(2):
-            first = keep.tile([N, HALF], F32, name="first%d" % h)
-            nc.scalar.copy(out=first[:], in_=banks[(0, h)][:])
-            lowest.append(first)
-        for m in range(1, 3):
-            for h in range(2):
-                lower = keep.tile([N, HALF], F32, name="lower%d_%d" % (m, h))
-                nc.vector.tensor_tensor(lower[:], banks[(m, h)][:], lowest[h][:], MIN)
-                lowest[h] = lower
+            one_pass(1, 0, h * HALF, QUARTER)
+            one_pass(1, 0, h * HALF + QUARTER, QUARTER)
+            one_pass(1, 1, h * HALF, HALF)
         for h in range(2):
-            nc.sync.dma_start(out=out[:, h * HALF : (h + 1) * HALF], in_=lowest[h][:])
+            for z in range(PASSES):
+                one_pass(z, 2, h * HALF, HALF)
+
+        copied = keep.tile([N, S], F32, name="copied")
+        for q in range(4):
+            nc.scalar.copy(out=copied[:, q * QUARTER : (q + 1) * QUARTER], in_=banks[(0, q * QUARTER)][:])
+        lower = keep.tile([N, S], F32, name="lower")
+        lowest = keep.tile([N, S], F32, name="lowest")
+
+        def lower_of(dst, src, m, first, width):
+            cols = slice(first, first + width)
+            bank_first = first // HALF * HALF
+            nc.vector.tensor_tensor(
+                dst[:, cols], banks[(m, bank_first)][:, first - bank_first : first - bank_first + width], src[:, cols], MIN
+            )
+
+        for q in range(4):
+            lower_of(lower, copied, 1, q * QUARTER, QUARTER)
+        for first, width in ((0, HALF), (HALF, QUARTER), (HALF + QUARTER, QUARTER)):
+            lower_of(lowest, lower, 2, first, width)
+            nc.sync.dma_start(out=out[:, first : first + width], in_=lowest[:, first : first + width])

@@ -34,35 +34,25 @@ def tile_picked_maxout_min_e_kernel(
         keep = ctx.enter_context(tc.tile_pool(name="keep", bufs=1))
         psum = ctx.enter_context(tc.psum_pool(name="psum", bufs=1))
 
-        pairs = [keep.tile([P, 2, T], F32, name="xpair%d" % u) for u in range(3)]
-        planes = [keep.tile([P, T], F32, name="xplane%d" % j) for j in range(2)]
+        ring = ctx.enter_context(tc.tile_pool(name="ring", bufs=3))
+        pairs = [ring.tile([P, 2, T], F32, name="xpair%d" % u, tag="ring", align_bytes=64) for u in range(3)]
         offsets = keep.tile([P, S // 16], U16, name="offsets")
         nc.sync.dma_start(out=pairs[0][:], in_=x_rows[0, :, 0:2, :])
         nc.sync.dma_start(offsets[:], offs)
-        nc.sync.dma_start(out=pairs[1][:], in_=x_rows[0, :, 2:4, :])
-        nc.sync.dma_start(out=pairs[2][:], in_=x_rows[1, :, 0:2, :])
-        for j in range(2):
-            nc.sync.dma_start(out=planes[j][:], in_=x_rows[1, :, 2 + j, :])
         wscale = keep.tile([P, PASSES, 3 * N], U8, name="wscale", align_bytes=64)
         nc.gpsimd.memset(wscale[:].bitcast(I32), 0)
         for m in range(3):
-            nc.gpsimd.dma_start(
+            nc.sync.dma_start(
                 out=wscale[0:16, :, m * N : (m + 1) * N].bitcast(I32),
                 in_=w_scales[m].rearrange("z r n -> r z n").bitcast(I32),
             )
+        nc.sync.dma_start(out=pairs[1][:], in_=x_rows[0, :, 2:4, :])
+        nc.sync.dma_start(out=pairs[2][:], in_=x_rows[1, :, 0:2, :])
         for q in range(1, 4):
             moved = slice(0, PASSES if q < 3 else 1)
-            nc.gpsimd.dma_start(
+            nc.scalar.dma_start(
                 out=wscale[32 * q : 32 * q + 4, moved, :].bitcast(I32), in_=wscale[4 * q : 4 * q + 4, moved, :].bitcast(I32)
             )
-
-        words = {}
-        for z, m in ((0, 0), (0, 1), (1, 0), (1, 1), (0, 2), (1, 2)):
-            wt = keep.tile([P, N], U32, name="wwords%d_%d" % (z, m), align_bytes=64)
-            nc.sync.dma_start(out=wt[:].bitcast(I32), in_=w_words[m][z].rearrange("p n t -> p (n t)").bitcast(I32))
-            words[(z, m)] = wt
-            if (z, m) == (1, 1):
-                nc.sync.dma_start(out=wscale[96:100, 1, :].bitcast(I32), in_=wscale[12:16, 1, :].bitcast(I32))
 
         def half_list(h):
             return offsets[:, h * LIST_COLS : (h + 1) * LIST_COLS]
@@ -70,6 +60,17 @@ def tile_picked_maxout_min_e_kernel(
         grouped0 = keep.tile([P, S, PACK], BF16, name="grouped0", align_bytes=64)
         for j in range(PACK):
             nc.vector.tensor_copy(grouped0[:, :, j], pairs[j // 2][:, j % 2, :].indirect(offsets[:]))
+
+        last_pair = ring.tile([P, 2, T], F32, name="xpair3", tag="ring", align_bytes=64)
+        for j in range(2):
+            nc.sync.dma_start(out=last_pair[:, j, :], in_=x_rows[1, :, 2 + j, :])
+        all_words = ring.tile([P, 3, PASSES, N], U32, name="wwords", tag="ring", align_bytes=64)
+        for z, m in ((0, 0), (0, 1), (1, 0), (1, 1), (0, 2), (1, 2)):
+            nc.sync.dma_start(
+                out=all_words[:, m, z, :].bitcast(I32), in_=w_words[m][z].rearrange("p n t -> p (n t)").bitcast(I32)
+            )
+            if (z, m) == (1, 1):
+                nc.sync.dma_start(out=wscale[96:100, 1, :].bitcast(I32), in_=wscale[12:16, 1, :].bitcast(I32))
 
         grouped1 = [keep.tile([P, HALF, PACK], BF16, name="grouped1_%d" % h, align_bytes=64) for h in range(2)]
         picked1 = keep.tile([P, 2, S], F32, name="picked1")
@@ -86,7 +87,7 @@ def tile_picked_maxout_min_e_kernel(
             )
         for j in range(2):
             for h in range(2):
-                nc.vector.tensor_copy(grouped1[h][:, :, 2 + j], planes[j][:].indirect(half_list(h)))
+                nc.vector.tensor_copy(grouped1[h][:, :, 2 + j], last_pair[:, j, :].indirect(half_list(h)))
 
         def w_scale(z, m):
             return wscale[:, z, m * N : (m + 1) * N]
@@ -110,7 +111,7 @@ def tile_picked_maxout_min_e_kernel(
             cols = slice(first, first + width)
             nc.tensor.matmul_mx(
                 out=banks[(m, first)][:],
-                lhsT=words[(z, m)][:].bitcast(FP8X4),
+                lhsT=all_words[:, m, z, :].bitcast(FP8X4),
                 lhsT_scale=w_scale(z, m),
                 rhs=codes[z][:, cols].bitcast(FP8X4),
                 rhs_scale=scales[z][:, cols],

@@ -50,7 +50,7 @@ def tile_picked_maxout_min_e_kernel(
         nc.sync.dma_start(out=pairs[2][:], in_=x_rows[1, :, 0:2, :])
         for q in range(1, 4):
             moved = slice(0, PASSES if q < 3 else 1)
-            nc.scalar.dma_start(
+            nc.sync.dma_start(
                 out=wscale[32 * q : 32 * q + 4, moved, :].bitcast(I32), in_=wscale[4 * q : 4 * q + 4, moved, :].bitcast(I32)
             )
 

@@ -20,6 +20,7 @@ PASSES = K // (P * PACK)
 HALF = S // 2
 QUARTER = S // 4
 LIST_COLS = HALF // 16
+WARM_M = 32
 
 
 def tile_picked_maxout_min_e_kernel(
@@ -48,6 +49,8 @@ def tile_picked_maxout_min_e_kernel(
             )
         nc.sync.dma_start(out=pairs[1][:], in_=x_rows[0, :, 2:4, :])
         nc.sync.dma_start(out=pairs[2][:], in_=x_rows[1, :, 0:2, :])
+        planes = [keep.tile([P, T], F32, name="xplane2")]
+        nc.sync.dma_start(out=planes[0][:], in_=x_rows[1, :, 2, :])
         for q in range(1, 4):
             moved = slice(0, PASSES if q < 3 else 1)
             nc.sync.dma_start(
@@ -61,9 +64,8 @@ def tile_picked_maxout_min_e_kernel(
         for j in range(PACK):
             nc.vector.tensor_copy(grouped0[:, :, j], pairs[j // 2][:, j % 2, :].indirect(offsets[:]))
 
-        last_pair = ring.tile([P, 2, T], F32, name="xpair3", tag="ring", align_bytes=64)
-        for j in range(2):
-            nc.sync.dma_start(out=last_pair[:, j, :], in_=x_rows[1, :, 2 + j, :])
+        planes.append(ring.tile([P, T], F32, name="xplane3", tag="ring", align_bytes=64))
+        nc.sync.dma_start(out=planes[1][:], in_=x_rows[1, :, 3, :])
         all_words = ring.tile([P, 3, PASSES, N], U32, name="wwords", tag="ring", align_bytes=64)
         for z, m in ((0, 0), (0, 1), (1, 0), (1, 1), (0, 2), (1, 2)):
             nc.sync.dma_start(
@@ -87,7 +89,7 @@ def tile_picked_maxout_min_e_kernel(
             )
         for j in range(2):
             for h in range(2):
-                nc.vector.tensor_copy(grouped1[h][:, :, 2 + j], last_pair[:, j, :].indirect(half_list(h)))
+                nc.vector.tensor_copy(grouped1[h][:, :, 2 + j], planes[j][:].indirect(half_list(h)))
 
         def w_scale(z, m):
             return wscale[:, z, m * N : (m + 1) * N]
@@ -105,7 +107,19 @@ def tile_picked_maxout_min_e_kernel(
         codes = (codes0, codes1)
         scales = (scales0, scales1)
         pieces = [(0, q * QUARTER, QUARTER) for q in range(4)] + [(m, h * HALF, HALF) for m in (1, 2) for h in range(2)]
-        banks = {(m, first): psum.tile([N, width], F32, name="bank%d_%d" % (m, first)) for m, first, width in pieces}
+        warm_bank = psum.tile([WARM_M, S], F32, name="warm_bank", tag="last")
+        for width in (S, S, QUARTER):
+            nc.tensor.matmul_mx(
+                out=warm_bank[:, 0:width],
+                lhsT=codes0[:, 0:WARM_M].bitcast(FP8X4),
+                lhsT_scale=wscale[:, 0, 0:WARM_M],
+                rhs=codes0[:, 0:width].bitcast(FP8X4),
+                rhs_scale=scales0[:, 0:width],
+                start=True,
+                stop=True,
+            )
+        banks = {(m, first): psum.tile([N, width], F32, name="bank%d_%d" % (m, first)) for m, first, width in pieces[:7]}
+        banks[(2, HALF)] = psum.tile([N, HALF], F32, name="bank_last", tag="last")
 
         def one_pass(z, m, first, width):
             cols = slice(first, first + width)

@@ -67,11 +67,11 @@ def tile_picked_maxout_min_e_kernel(
         planes.append(ring.tile([P, T], F32, name="xplane3", tag="ring", align_bytes=64))
         nc.sync.dma_start(out=planes[1][:], in_=x_rows[1, :, 3, :])
         all_words = ring.tile([P, 3, PASSES, N], U32, name="wwords", tag="ring", align_bytes=64)
-        for z, m in ((0, 0), (0, 1), (1, 0), (1, 1), (0, 2), (1, 2)):
+        for z, m in ((0, 0), (0, 1), (0, 2), (1, 0), (1, 1), (1, 2)):
             nc.sync.dma_start(
                 out=all_words[:, m, z, :].bitcast(I32), in_=w_words[m][z].rearrange("p n t -> p (n t)").bitcast(I32)
             )
-            if (z, m) == (1, 1):
+            if (z, m) == (1, 2):
                 nc.sync.dma_start(out=wscale[96:100, 1, :].bitcast(I32), in_=wscale[12:16, 1, :].bitcast(I32))
 
         grouped1 = [keep.tile([P, HALF, PACK], BF16, name="grouped1_%d" % h, align_bytes=64) for h in range(2)]
@@ -133,15 +133,16 @@ def tile_picked_maxout_min_e_kernel(
                 stop=z == PASSES - 1,
             )
 
-        for m, first, width in pieces[:6]:
+        for m, first, width in pieces:
             one_pass(0, m, first, width)
-        for h in range(2):
-            one_pass(1, 0, h * HALF, QUARTER)
-            one_pass(1, 0, h * HALF + QUARTER, QUARTER)
-            one_pass(1, 1, h * HALF, HALF)
-        for h in range(2):
-            for z in range(PASSES):
-                one_pass(z, 2, h * HALF, HALF)
+        one_pass(1, 0, 0, QUARTER)
+        one_pass(1, 0, QUARTER, QUARTER)
+        one_pass(1, 1, 0, HALF)
+        one_pass(1, 0, HALF, QUARTER)
+        one_pass(1, 2, 0, HALF)
+        one_pass(1, 0, HALF + QUARTER, QUARTER)
+        one_pass(1, 1, HALF, HALF)
+        one_pass(1, 2, HALF, HALF)
 
         copied = keep.tile([N, S], F32, name="copied")
         for q in range(4):
@@ -156,8 +157,13 @@ def tile_picked_maxout_min_e_kernel(
                 dst[:, cols], banks[(m, bank_first)][:, first - bank_first : first - bank_first + width], src[:, cols], MIN
             )
 
-        for q in range(4):
-            lower_of(lower, copied, 1, q * QUARTER, QUARTER)
-        for first, width in ((0, HALF), (HALF, QUARTER), (HALF + QUARTER, QUARTER)):
+        def finish(first, width):
             lower_of(lowest, lower, 2, first, width)
             nc.sync.dma_start(out=out[:, first : first + width], in_=lowest[:, first : first + width])
+
+        for q in range(3):
+            lower_of(lower, copied, 1, q * QUARTER, QUARTER)
+        finish(0, QUARTER)
+        lower_of(lower, copied, 1, 3 * QUARTER, QUARTER)
+        for q in range(1, 4):
+            finish(q * QUARTER, QUARTER)

@@ -13,6 +13,7 @@ U16 = mybir.dt.uint16
 U8 = mybir.dt.uint8
 FP8X4 = mybir.dt.float8_e4m3fn_x4
 MIN = mybir.AluOpType.min
+COPY = mybir.ActivationFunctionType.Copy
 
 P = 128
 PACK = 4
@@ -60,6 +61,9 @@ def tile_picked_maxout_min_e_kernel(
         def half_list(h):
             return offsets[:, h * LIST_COLS : (h + 1) * LIST_COLS]
 
+        def quarter_list(q):
+            return offsets[:, q * LIST_COLS // 2 : (q + 1) * LIST_COLS // 2]
+
         grouped0 = keep.tile([P, S, PACK], BF16, name="grouped0", align_bytes=64)
         for j in range(PACK):
             nc.vector.tensor_copy(grouped0[:, :, j], pairs[j // 2][:, j % 2, :].indirect(offsets[:]))
@@ -71,7 +75,7 @@ def tile_picked_maxout_min_e_kernel(
             nc.sync.dma_start(
                 out=all_words[:, m, z, :].bitcast(I32), in_=w_words[m][z].rearrange("p n t -> p (n t)").bitcast(I32)
             )
-            if (z, m) == (1, 2):
+            if (z, m) == (1, 1):
                 nc.sync.dma_start(out=wscale[96:100, 1, :].bitcast(I32), in_=wscale[12:16, 1, :].bitcast(I32))
 
         grouped1 = [keep.tile([P, HALF, PACK], BF16, name="grouped1_%d" % h, align_bytes=64) for h in range(2)]
@@ -87,9 +91,17 @@ def tile_picked_maxout_min_e_kernel(
             nc.scalar.copy(
                 out=grouped1[h][:, :, 0:2], in_=picked1[:, :, h * HALF : (h + 1) * HALF].rearrange("p j s -> p s j")
             )
-        for j in range(2):
-            for h in range(2):
-                nc.vector.tensor_copy(grouped1[h][:, :, 2 + j], planes[j][:].indirect(half_list(h)))
+        late = keep.tile([P, 2, HALF], BF16, name="late", align_bytes=64)
+        nc.vector.tensor_copy(grouped1[0][:, :, 2], planes[0][:].indirect(half_list(0)))
+        nc.vector.tensor_copy(late[:, 0, :], planes[0][:].indirect(half_list(1)))
+        nc.vector.tensor_copy(grouped1[0][:, :, 3], planes[1][:].indirect(half_list(0)))
+        nc.scalar.activation(late[:, 1, 0:QUARTER], planes[1][:].indirect(quarter_list(2)), COPY)
+        nc.vector.tensor_copy(late[:, 1, QUARTER:HALF], planes[1][:].indirect(quarter_list(3)))
+        for first in (0, QUARTER):
+            nc.scalar.copy(
+                out=grouped1[1][:, first : first + QUARTER, 2:4],
+                in_=late[:, :, first : first + QUARTER].rearrange("p j s -> p s j"),
+            )
 
         def w_scale(z, m):
             return wscale[:, z, m * N : (m + 1) * N]
@@ -106,7 +118,6 @@ def tile_picked_maxout_min_e_kernel(
 
         codes = (codes0, codes1)
         scales = (scales0, scales1)
-        pieces = [(0, q * QUARTER, QUARTER) for q in range(4)] + [(m, h * HALF, HALF) for m in (1, 2) for h in range(2)]
         warm_bank = psum.tile([WARM_M, S], F32, name="warm_bank", tag="last")
         for width in (S, S, QUARTER):
             nc.tensor.matmul_mx(
@@ -118,52 +129,72 @@ def tile_picked_maxout_min_e_kernel(
                 start=True,
                 stop=True,
             )
-        banks = {(m, first): psum.tile([N, width], F32, name="bank%d_%d" % (m, first)) for m, first, width in pieces[:7]}
-        banks[(2, HALF)] = psum.tile([N, HALF], F32, name="bank_last", tag="last")
 
-        def one_pass(z, m, first, width):
+        first_bank = [psum.tile([N, QUARTER], F32, name="first%d" % q) for q in range(4)]
+        early_bank = {1: psum.tile([N, HALF], F32, name="second_early")}
+        early_bank[2] = psum.tile([N, HALF], F32, name="third_early", tag="last")
+        late_bank = {q: psum.tile([N, 2, QUARTER], F32, name="late%d" % q) for q in (2, 3)}
+
+        def multiply(bank, z, m, first, width, start, stop):
             cols = slice(first, first + width)
             nc.tensor.matmul_mx(
-                out=banks[(m, first)][:],
+                out=bank,
                 lhsT=all_words[:, m, z, :].bitcast(FP8X4),
                 lhsT_scale=w_scale(z, m),
                 rhs=codes[z][:, cols].bitcast(FP8X4),
                 rhs_scale=scales[z][:, cols],
-                start=z == 0,
-                stop=z == PASSES - 1,
+                start=start,
+                stop=stop,
             )
 
-        for m, first, width in pieces:
-            one_pass(0, m, first, width)
-        one_pass(1, 0, 0, QUARTER)
-        one_pass(1, 0, QUARTER, QUARTER)
-        one_pass(1, 1, 0, HALF)
-        one_pass(1, 0, HALF, QUARTER)
-        one_pass(1, 2, 0, HALF)
-        one_pass(1, 0, HALF + QUARTER, QUARTER)
-        one_pass(1, 1, HALF, HALF)
-        one_pass(1, 2, HALF, HALF)
+        def first_product(z, q):
+            multiply(first_bank[q][:], z, 0, q * QUARTER, QUARTER, z == 0, z == 1)
+
+        def early_half(z, m):
+            multiply(early_bank[m][:], z, m, 0, HALF, z == 0, z == 1)
+
+        def late_quarter(z, m, q):
+            multiply(late_bank[q][:, m - 1, :], z, m, q * QUARTER, QUARTER, (z, m) == (0, 1), (z, m) == (1, 2))
+
+        for q in range(4):
+            first_product(0, q)
+        for m in (1, 2):
+            early_half(0, m)
+            for q in (2, 3):
+                late_quarter(0, m, q)
+        first_product(1, 0)
+        first_product(1, 1)
+        early_half(1, 1)
+        first_product(1, 2)
+        late_quarter(1, 1, 2)
+        late_quarter(1, 2, 2)
+        first_product(1, 3)
+        early_half(1, 2)
+        late_quarter(1, 1, 3)
+        late_quarter(1, 2, 3)
 
         copied = keep.tile([N, S], F32, name="copied")
-        for q in range(4):
-            nc.scalar.copy(out=copied[:, q * QUARTER : (q + 1) * QUARTER], in_=banks[(0, q * QUARTER)][:])
         lower = keep.tile([N, S], F32, name="lower")
         lowest = keep.tile([N, S], F32, name="lowest")
 
-        def lower_of(dst, src, m, first, width):
-            cols = slice(first, first + width)
-            bank_first = first // HALF * HALF
-            nc.vector.tensor_tensor(
-                dst[:, cols], banks[(m, bank_first)][:, first - bank_first : first - bank_first + width], src[:, cols], MIN
-            )
+        def quarter(q):
+            return slice(q * QUARTER, (q + 1) * QUARTER)
 
-        def finish(first, width):
-            lower_of(lowest, lower, 2, first, width)
-            nc.sync.dma_start(out=out[:, first : first + width], in_=lowest[:, first : first + width])
+        def product(m, q):
+            return early_bank[m][:, quarter(q)] if q < 2 else late_bank[q][:, m - 1, :]
 
+        def first_minimum(q):
+            nc.vector.tensor_tensor(lower[:, quarter(q)], product(1, q), copied[:, quarter(q)], MIN)
+
+        def finish(q):
+            nc.vector.tensor_tensor(lowest[:, quarter(q)], product(2, q), lower[:, quarter(q)], MIN)
+            nc.sync.dma_start(out=out[:, quarter(q)], in_=lowest[:, quarter(q)])
+
+        for q in range(4):
+            nc.scalar.copy(out=copied[:, quarter(q)], in_=first_bank[q][:])
         for q in range(3):
-            lower_of(lower, copied, 1, q * QUARTER, QUARTER)
-        finish(0, QUARTER)
-        lower_of(lower, copied, 1, 3 * QUARTER, QUARTER)
+            first_minimum(q)
+        finish(0)
+        first_minimum(3)
         for q in range(1, 4):
-            finish(q * QUARTER, QUARTER)
+            finish(q)

@@ -21,7 +21,6 @@ PASSES = K // (P * PACK)
 HALF = S // 2
 QUARTER = S // 4
 LIST_COLS = HALF // 16
-WARM_M = 32
 
 
 def tile_picked_maxout_min_e_kernel(
@@ -118,21 +117,10 @@ def tile_picked_maxout_min_e_kernel(
 
         codes = (codes0, codes1)
         scales = (scales0, scales1)
-        warm_bank = psum.tile([WARM_M, S], F32, name="warm_bank", tag="last")
-        for width in (S, S, QUARTER):
-            nc.tensor.matmul_mx(
-                out=warm_bank[:, 0:width],
-                lhsT=codes0[:, 0:WARM_M].bitcast(FP8X4),
-                lhsT_scale=wscale[:, 0, 0:WARM_M],
-                rhs=codes0[:, 0:width].bitcast(FP8X4),
-                rhs_scale=scales0[:, 0:width],
-                start=True,
-                stop=True,
-            )
 
         first_bank = [psum.tile([N, QUARTER], F32, name="first%d" % q) for q in range(4)]
         early_bank = {1: psum.tile([N, HALF], F32, name="second_early")}
-        early_bank[2] = psum.tile([N, HALF], F32, name="third_early", tag="last")
+        early_bank[2] = psum.tile([N, HALF], F32, name="third_early")
         late_bank = {q: psum.tile([N, 2, QUARTER], F32, name="late%d" % q) for q in (2, 3)}
 
         def multiply(bank, z, m, first, width, start, stop):

@@ -118,10 +118,12 @@ def tile_picked_maxout_min_e_kernel(
         codes = (codes0, codes1)
         scales = (scales0, scales1)
 
-        first_bank = [psum.tile([N, QUARTER], F32, name="first%d" % q) for q in range(4)]
-        early_bank = {1: psum.tile([N, HALF], F32, name="second_early")}
-        early_bank[2] = psum.tile([N, HALF], F32, name="third_early")
-        late_bank = {q: psum.tile([N, 2, QUARTER], F32, name="late%d" % q) for q in (2, 3)}
+        banks = [
+            [(q * QUARTER, QUARTER, psum.tile([N, QUARTER], F32, name="first%d" % q, tag="bank%d" % q)) for q in range(4)],
+            [(q * QUARTER, QUARTER, psum.tile([N, QUARTER], F32, name="second%d" % q)) for q in range(2)],
+            [(0, HALF, psum.tile([N, HALF], F32, name="third_early"))],
+        ]
+        banks[1].append((HALF, HALF, psum.tile([N, HALF], F32, name="second_late")))
 
         def multiply(bank, z, m, first, width, start, stop):
             cols = slice(first, first + width)
@@ -135,31 +137,15 @@ def tile_picked_maxout_min_e_kernel(
                 stop=stop,
             )
 
-        def first_product(z, q):
-            multiply(first_bank[q][:], z, 0, q * QUARTER, QUARTER, z == 0, z == 1)
+        def one_pass(z, m, piece):
+            first, width, bank = banks[m][piece]
+            multiply(bank[:], z, m, first, width, z == 0, z == 1)
 
-        def early_half(z, m):
-            multiply(early_bank[m][:], z, m, 0, HALF, z == 0, z == 1)
-
-        def late_quarter(z, m, q):
-            multiply(late_bank[q][:, m - 1, :], z, m, q * QUARTER, QUARTER, (z, m) == (0, 1), (z, m) == (1, 2))
-
-        for q in range(4):
-            first_product(0, q)
-        for m in (1, 2):
-            early_half(0, m)
-            for q in (2, 3):
-                late_quarter(0, m, q)
-        first_product(1, 0)
-        first_product(1, 1)
-        early_half(1, 1)
-        first_product(1, 2)
-        late_quarter(1, 1, 2)
-        late_quarter(1, 2, 2)
-        first_product(1, 3)
-        early_half(1, 2)
-        late_quarter(1, 1, 3)
-        late_quarter(1, 2, 3)
+        for m in range(3):
+            for piece in range(len(banks[m])):
+                one_pass(0, m, piece)
+        for m, piece in ((0, 0), (0, 1), (1, 0), (0, 2), (1, 1), (0, 3), (1, 2), (2, 0)):
+            one_pass(1, m, piece)
 
         copied = keep.tile([N, S], F32, name="copied")
         lower = keep.tile([N, S], F32, name="lower")
@@ -168,8 +154,16 @@ def tile_picked_maxout_min_e_kernel(
         def quarter(q):
             return slice(q * QUARTER, (q + 1) * QUARTER)
 
+        for q in range(4):
+            nc.scalar.copy(out=copied[:, quarter(q)], in_=banks[0][q][2][:])
+        for q in (2, 3):
+            banks[2].append((q * QUARTER, QUARTER, psum.tile([N, QUARTER], F32, name="third%d" % q, tag="bank%d" % (q - 2))))
+            for z in range(PASSES):
+                one_pass(z, 2, q - 1)
+
         def product(m, q):
-            return early_bank[m][:, quarter(q)] if q < 2 else late_bank[q][:, m - 1, :]
+            first, width, bank = [piece for piece in banks[m] if piece[0] <= q * QUARTER < piece[0] + piece[1]][0]
+            return bank[:, q * QUARTER - first : (q + 1) * QUARTER - first]
 
         def first_minimum(q):
             nc.vector.tensor_tensor(lower[:, quarter(q)], product(1, q), copied[:, quarter(q)], MIN)
@@ -178,8 +172,6 @@ def tile_picked_maxout_min_e_kernel(
             nc.vector.tensor_tensor(lowest[:, quarter(q)], product(2, q), lower[:, quarter(q)], MIN)
             nc.sync.dma_start(out=out[:, quarter(q)], in_=lowest[:, quarter(q)])
 
-        for q in range(4):
-            nc.scalar.copy(out=copied[:, quarter(q)], in_=first_bank[q][:])
         for q in range(3):
             first_minimum(q)
         finish(0)

@@ -52,10 +52,7 @@ def tile_picked_maxout_min_e_kernel(
         planes = [keep.tile([P, T], F32, name="xplane2")]
         nc.sync.dma_start(out=planes[0][:], in_=x_rows[1, :, 2, :])
         for q in range(1, 4):
-            moved = slice(0, PASSES if q < 3 else 1)
-            nc.sync.dma_start(
-                out=wscale[32 * q : 32 * q + 4, moved, :].bitcast(I32), in_=wscale[4 * q : 4 * q + 4, moved, :].bitcast(I32)
-            )
+            nc.sync.dma_start(out=wscale[32 * q : 32 * q + 4].bitcast(I32), in_=wscale[4 * q : 4 * q + 4].bitcast(I32))
 
         def half_list(h):
             return offsets[:, h * LIST_COLS : (h + 1) * LIST_COLS]
@@ -70,12 +67,13 @@ def tile_picked_maxout_min_e_kernel(
         planes.append(ring.tile([P, T], F32, name="xplane3", tag="ring", align_bytes=64))
         nc.sync.dma_start(out=planes[1][:], in_=x_rows[1, :, 3, :])
         all_words = ring.tile([P, 3, PASSES, N], U32, name="wwords", tag="ring", align_bytes=64)
-        for z, m in ((0, 0), (0, 1), (0, 2), (1, 0), (1, 1), (1, 2)):
+        for z, m in ((0, 0), (0, 1), (1, 0), (1, 1)):
             nc.sync.dma_start(
                 out=all_words[:, m, z, :].bitcast(I32), in_=w_words[m][z].rearrange("p n t -> p (n t)").bitcast(I32)
             )
-            if (z, m) == (1, 1):
-                nc.sync.dma_start(out=wscale[96:100, 1, :].bitcast(I32), in_=wscale[12:16, 1, :].bitcast(I32))
+        nc.sync.dma_start(
+            out=all_words[:, 2, :, :].bitcast(I32), in_=w_words[2].rearrange("z p n t -> p z (n t)").bitcast(I32)
+        )
 
         grouped1 = [keep.tile([P, HALF, PACK], BF16, name="grouped1_%d" % h, align_bytes=64) for h in range(2)]
         picked1 = keep.tile([P, 2, S], F32, name="picked1")
@@ -118,12 +116,16 @@ def tile_picked_maxout_min_e_kernel(
         codes = (codes0, codes1)
         scales = (scales0, scales1)
 
-        banks = [
-            [(q * QUARTER, QUARTER, psum.tile([N, QUARTER], F32, name="first%d" % q, tag="bank%d" % q)) for q in range(4)],
-            [(q * QUARTER, QUARTER, psum.tile([N, QUARTER], F32, name="second%d" % q)) for q in range(2)],
-            [(0, HALF, psum.tile([N, HALF], F32, name="third_early"))],
-        ]
-        banks[1].append((HALF, HALF, psum.tile([N, HALF], F32, name="second_late")))
+        place = {(m, q): psum.tile([N, QUARTER], F32, name="own%d_%d" % (m, q))[:] for m in range(2) for q in range(2)}
+        two = psum.tile([N, 2, QUARTER], F32, name="two")
+        three = psum.tile([N, 3, QUARTER], F32, name="three")
+        third_early = psum.tile([N, HALF], F32, name="third_early")
+        for m in range(2):
+            place[m, 2] = two[:, m, :]
+            place[2, m] = third_early[:, m * QUARTER : (m + 1) * QUARTER]
+        for m in range(3):
+            place[m, 3] = three[:, m, :]
+        place[2, 2] = psum.tile([N, QUARTER], F32, name="third_late")[:]
 
         def multiply(bank, z, m, first, width, start, stop):
             cols = slice(first, first + width)
@@ -137,44 +139,40 @@ def tile_picked_maxout_min_e_kernel(
                 stop=stop,
             )
 
-        def one_pass(z, m, piece):
-            first, width, bank = banks[m][piece]
-            multiply(bank[:], z, m, first, width, z == 0, z == 1)
+        def one_pass(z, m, q):
+            shared = q == 3 or (q == 2 and m < 2)
+            opens = z == 0 and (m == 0 or not shared)
+            closes = z == 1 and (not shared or m == (2 if q == 3 else 0))
+            multiply(place[m, q], z, m, q * QUARTER, QUARTER, opens, closes)
 
+        for m in range(2):
+            for q in range(4):
+                one_pass(0, m, q)
+        for m, q in ((0, 0), (0, 1), (1, 0), (1, 2), (0, 2), (1, 1)):
+            one_pass(1, m, q)
+        for z in range(PASSES):
+            multiply(third_early[:], z, 2, 0, HALF, z == 0, z == 1)
+        for z in range(PASSES):
+            one_pass(z, 2, 2)
+        one_pass(0, 2, 3)
         for m in range(3):
-            for piece in range(len(banks[m])):
-                one_pass(0, m, piece)
-        for m, piece in ((0, 0), (0, 1), (1, 0), (0, 2), (1, 1), (0, 3), (1, 2), (2, 0)):
-            one_pass(1, m, piece)
+            one_pass(1, m, 3)
 
-        copied = keep.tile([N, S], F32, name="copied")
-        lower = keep.tile([N, S], F32, name="lower")
+        copied = keep.tile([N, 3 * QUARTER], F32, name="copied")
+        lower = keep.tile([N, 3 * QUARTER], F32, name="lower")
         lowest = keep.tile([N, S], F32, name="lowest")
 
         def quarter(q):
             return slice(q * QUARTER, (q + 1) * QUARTER)
 
-        for q in range(4):
-            nc.scalar.copy(out=copied[:, quarter(q)], in_=banks[0][q][2][:])
-        for q in (2, 3):
-            banks[2].append((q * QUARTER, QUARTER, psum.tile([N, QUARTER], F32, name="third%d" % q, tag="bank%d" % (q - 2))))
-            for z in range(PASSES):
-                one_pass(z, 2, q - 1)
-
-        def product(m, q):
-            first, width, bank = [piece for piece in banks[m] if piece[0] <= q * QUARTER < piece[0] + piece[1]][0]
-            return bank[:, q * QUARTER - first : (q + 1) * QUARTER - first]
-
-        def first_minimum(q):
-            nc.vector.tensor_tensor(lower[:, quarter(q)], product(1, q), copied[:, quarter(q)], MIN)
-
-        def finish(q):
-            nc.vector.tensor_tensor(lowest[:, quarter(q)], product(2, q), lower[:, quarter(q)], MIN)
-            nc.sync.dma_start(out=out[:, quarter(q)], in_=lowest[:, quarter(q)])
-
         for q in range(3):
-            first_minimum(q)
-        finish(0)
-        first_minimum(3)
-        for q in range(1, 4):
-            finish(q)
+            nc.scalar.copy(out=copied[:, quarter(q)], in_=place[0, q])
+            nc.vector.tensor_tensor(lower[:, quarter(q)], place[1, q], copied[:, quarter(q)], MIN)
+        for q in range(4):
+            if q < 3:
+                nc.vector.tensor_tensor(lowest[:, quarter(q)], place[2, q], lower[:, quarter(q)], MIN)
+            else:
+                nc.vector.tensor_reduce(
+                    out=lowest[:, quarter(q)], in_=three[:].rearrange("p m s -> p s m"), axis=mybir.AxisListType.X, op=MIN
+                )
+            nc.sync.dma_start(out=out[:, quarter(q)], in_=lowest[:, quarter(q)])

@@ -20,7 +20,7 @@ PACK = 4
 PASSES = K // (P * PACK)
 HALF = S // 2
 QUARTER = S // 4
-LIST_COLS = HALF // 16
+PAIR_BYTES = 2 * T * 4
 
 
 def tile_picked_maxout_min_e_kernel(
@@ -33,10 +33,19 @@ def tile_picked_maxout_min_e_kernel(
 
     with ExitStack() as ctx:
         keep = ctx.enter_context(tc.tile_pool(name="keep", bufs=1))
+        reuse = ctx.enter_context(tc.tile_pool(name="reuse", bufs=1))
         psum = ctx.enter_context(tc.psum_pool(name="psum", bufs=1))
 
-        ring = ctx.enter_context(tc.tile_pool(name="ring", bufs=3))
-        pairs = [ring.tile([P, 2, T], F32, name="xpair%d" % u, tag="ring", align_bytes=64) for u in range(3)]
+        def entries(first, count):
+            return offsets[:, first // 16 : (first + count) // 16]
+
+        def quarter(q):
+            return slice(q * QUARTER, (q + 1) * QUARTER)
+
+        def load_words(dst, m, z):
+            nc.sync.dma_start(out=dst.bitcast(I32), in_=w_words[m][z].rearrange("p n t -> p (n t)").bitcast(I32))
+
+        pairs = [reuse.tile([P, 2, T], F32, name="xpair%d" % u, offset=u * PAIR_BYTES, align_bytes=64) for u in range(3)]
         offsets = keep.tile([P, S // 16], U16, name="offsets")
         nc.sync.dma_start(out=pairs[0][:], in_=x_rows[0, :, 0:2, :])
         nc.sync.dma_start(offsets[:], offs)
@@ -49,39 +58,40 @@ def tile_picked_maxout_min_e_kernel(
             )
         nc.sync.dma_start(out=pairs[1][:], in_=x_rows[0, :, 2:4, :])
         nc.sync.dma_start(out=pairs[2][:], in_=x_rows[1, :, 0:2, :])
-        planes = [keep.tile([P, T], F32, name="xplane2")]
-        nc.sync.dma_start(out=planes[0][:], in_=x_rows[1, :, 2, :])
+        plane2 = keep.tile([P, T], F32, name="xplane2", align_bytes=64)
+        nc.sync.dma_start(out=plane2[:], in_=x_rows[1, :, 2, :])
         for q in range(1, 4):
-            nc.sync.dma_start(out=wscale[32 * q : 32 * q + 4].bitcast(I32), in_=wscale[4 * q : 4 * q + 4].bitcast(I32))
-
-        def half_list(h):
-            return offsets[:, h * LIST_COLS : (h + 1) * LIST_COLS]
-
-        def quarter_list(q):
-            return offsets[:, q * LIST_COLS // 2 : (q + 1) * LIST_COLS // 2]
+            nc.sync.dma_start(
+                out=wscale[32 * q : 32 * q + 4, 0, :].bitcast(I32), in_=wscale[4 * q : 4 * q + 4, 0, :].bitcast(I32)
+            )
 
         grouped0 = keep.tile([P, S, PACK], BF16, name="grouped0", align_bytes=64)
         for j in range(PACK):
             nc.vector.tensor_copy(grouped0[:, :, j], pairs[j // 2][:, j % 2, :].indirect(offsets[:]))
 
-        planes.append(ring.tile([P, T], F32, name="xplane3", tag="ring", align_bytes=64))
-        nc.sync.dma_start(out=planes[1][:], in_=x_rows[1, :, 3, :])
-        all_words = ring.tile([P, 3, PASSES, N], U32, name="wwords", tag="ring", align_bytes=64)
-        for z, m in ((0, 0), (0, 1), (1, 0), (1, 1)):
-            nc.sync.dma_start(
-                out=all_words[:, m, z, :].bitcast(I32), in_=w_words[m][z].rearrange("p n t -> p (n t)").bitcast(I32)
-            )
+        plane3 = reuse.tile([P, T], F32, name="xplane3", offset=0, align_bytes=64)
+        nc.sync.dma_start(out=plane3[:, 0 : T // 2], in_=x_rows[1, :, 3, 0 : T // 2])
+        early_words = reuse.tile([P, 2, N], U32, name="early_words", offset=PAIR_BYTES // 2, align_bytes=64)
+        for m in range(2):
+            load_words(early_words[:, m, :], m, 0)
+        nc.sync.dma_start(out=plane3[:, T // 2 : T], in_=x_rows[1, :, 3, T // 2 : T])
+        late_bytes = reuse.tile([P, 4 * PACK * N + 3 * N], U8, name="late_bytes", offset=PAIR_BYTES, align_bytes=64)
+        late_words = late_bytes[:, 0 : 4 * PACK * N].bitcast(U32).rearrange("p (a n) -> p a n", a=4)
+        wscale1 = late_bytes[:, 4 * PACK * N :]
+        nc.vector.memset(wscale1.bitcast(I32), 0)
         nc.sync.dma_start(
-            out=all_words[:, 2, :, :].bitcast(I32), in_=w_words[2].rearrange("z p n t -> p z (n t)").bitcast(I32)
+            out=late_words[:, 0:2, :].bitcast(I32), in_=w_words[2].rearrange("z p n t -> p z (n t)").bitcast(I32)
         )
+        for m in range(2):
+            load_words(late_words[:, 2 + m, :], m, 1)
+        for q in range(4):
+            nc.sync.dma_start(out=wscale1[32 * q : 32 * q + 4].bitcast(I32), in_=wscale[4 * q : 4 * q + 4, 1, :].bitcast(I32))
+        w_planes = (wscale[:, 0, :], wscale1)
+        words = {(0, 0): early_words[:, 0, :], (0, 1): early_words[:, 1, :], (0, 2): late_words[:, 0, :]}
+        words.update({(1, 2): late_words[:, 1, :], (1, 0): late_words[:, 2, :], (1, 1): late_words[:, 3, :]})
 
         grouped1 = [keep.tile([P, HALF, PACK], BF16, name="grouped1_%d" % h, align_bytes=64) for h in range(2)]
         picked1 = keep.tile([P, 2, S], F32, name="picked1")
-        codes0 = keep.tile([P, S], U32, name="codes0", align_bytes=64)
-        scales0 = keep.tile([P, S], U8, name="scales0", align_bytes=64)
-        nc.vector.quantize_mx(
-            out=codes0[:].bitcast(FP8X4), scales=scales0[:], in_=grouped0[:].rearrange("p s j -> p (s j)")
-        )
         for e in range(2):
             nc.vector.tensor_copy(picked1[:, e, :], pairs[2][:, e, :].indirect(offsets[:]))
         for h in range(2):
@@ -89,90 +99,75 @@ def tile_picked_maxout_min_e_kernel(
                 out=grouped1[h][:, :, 0:2], in_=picked1[:, :, h * HALF : (h + 1) * HALF].rearrange("p j s -> p s j")
             )
         late = keep.tile([P, 2, HALF], BF16, name="late", align_bytes=64)
-        nc.vector.tensor_copy(grouped1[0][:, :, 2], planes[0][:].indirect(half_list(0)))
-        nc.vector.tensor_copy(late[:, 0, :], planes[0][:].indirect(half_list(1)))
-        nc.vector.tensor_copy(grouped1[0][:, :, 3], planes[1][:].indirect(half_list(0)))
-        nc.scalar.activation(late[:, 1, 0:QUARTER], planes[1][:].indirect(quarter_list(2)), COPY)
-        nc.vector.tensor_copy(late[:, 1, QUARTER:HALF], planes[1][:].indirect(quarter_list(3)))
-        for first in (0, QUARTER):
-            nc.scalar.copy(
-                out=grouped1[1][:, first : first + QUARTER, 2:4],
-                in_=late[:, :, first : first + QUARTER].rearrange("p j s -> p s j"),
-            )
+        nc.vector.tensor_copy(grouped1[0][:, :, 2], plane2[:].indirect(entries(0, HALF)))
+        nc.vector.tensor_copy(late[:, 0, :], plane2[:].indirect(entries(HALF, HALF)))
 
-        def w_scale(z, m):
-            return wscale[:, z, m * N : (m + 1) * N]
+        codes0 = keep.tile([P, S], U32, name="codes0", align_bytes=64)
+        scales0 = keep.tile([P, S], U8, name="scales0", align_bytes=64)
+        nc.vector.quantize_mx(
+            out=codes0[:].bitcast(FP8X4), scales=scales0[:], in_=grouped0[:].rearrange("p s j -> p (s j)")
+        )
+
+        nc.vector.tensor_copy(grouped1[0][:, :, 3], plane3[:].indirect(entries(0, HALF)))
+        nc.scalar.activation(late[:, 1, 0:QUARTER], plane3[:].indirect(entries(HALF, QUARTER)), COPY)
+        nc.vector.tensor_copy(late[:, 1, QUARTER:HALF], plane3[:].indirect(entries(HALF + QUARTER, QUARTER)))
+        for q in range(2):
+            nc.scalar.copy(out=grouped1[1][:, quarter(q), 2:4], in_=late[:, :, quarter(q)].rearrange("p j s -> p s j"))
 
         codes1 = keep.tile([P, S], U32, name="codes1", align_bytes=64)
         scales1 = keep.tile([P, S], U8, name="scales1", align_bytes=64)
-        for h, first, width in [(h, q * QUARTER, QUARTER) for h in range(2) for q in range(2)]:
-            cols = slice(h * HALF + first, h * HALF + first + width)
+        for q in range(4):
             nc.vector.quantize_mx(
-                out=codes1[:, cols].bitcast(FP8X4),
-                scales=scales1[:, cols],
-                in_=grouped1[h][:, first : first + width, :].rearrange("p s j -> p (s j)"),
+                out=codes1[:, quarter(q)].bitcast(FP8X4),
+                scales=scales1[:, quarter(q)],
+                in_=grouped1[q // 2][:, quarter(q % 2), :].rearrange("p s j -> p (s j)"),
             )
-
         codes = (codes0, codes1)
         scales = (scales0, scales1)
 
-        place = {(m, q): psum.tile([N, QUARTER], F32, name="own%d_%d" % (m, q))[:] for m in range(2) for q in range(2)}
-        two = psum.tile([N, 2, QUARTER], F32, name="two")
-        three = psum.tile([N, 3, QUARTER], F32, name="three")
-        third_early = psum.tile([N, HALF], F32, name="third_early")
-        for m in range(2):
-            place[m, 2] = two[:, m, :]
-            place[2, m] = third_early[:, m * QUARTER : (m + 1) * QUARTER]
-        for m in range(3):
-            place[m, 3] = three[:, m, :]
-        place[2, 2] = psum.tile([N, QUARTER], F32, name="third_late")[:]
+        trio = {q: psum.tile([N, 3, QUARTER], F32, name="trio%d" % q) for q in (0, 3)}
+        lone = {q: psum.tile([N, QUARTER], F32, name="lone%d" % q) for q in (1, 2)}
+        duo = {q: psum.tile([N, 2, QUARTER], F32, name="duo%d" % q) for q in (1, 2)}
 
-        def multiply(bank, z, m, first, width, start, stop):
-            cols = slice(first, first + width)
-            nc.tensor.matmul_mx(
-                out=bank,
-                lhsT=all_words[:, m, z, :].bitcast(FP8X4),
-                lhsT_scale=w_scale(z, m),
-                rhs=codes[z][:, cols].bitcast(FP8X4),
-                rhs_scale=scales[z][:, cols],
-                start=start,
-                stop=stop,
-            )
+        def place(m, q):
+            if q in trio:
+                return trio[q][:, m, :]
+            return lone[q][:] if m == 1 else duo[q][:, m // 2, :]
 
         def one_pass(z, m, q):
-            shared = q == 3 or (q == 2 and m < 2)
-            opens = z == 0 and (m == 0 or not shared)
-            closes = z == 1 and (not shared or m == (2 if q == 3 else 0))
-            multiply(place[m, q], z, m, q * QUARTER, QUARTER, opens, closes)
+            alone = q in lone and m == 1
+            nc.tensor.matmul_mx(
+                out=place(m, q),
+                lhsT=words[z, m].bitcast(FP8X4),
+                lhsT_scale=w_planes[z][:, m * N : (m + 1) * N],
+                rhs=codes[z][:, quarter(q)].bitcast(FP8X4),
+                rhs_scale=scales[z][:, quarter(q)],
+                start=z == 0 and (alone or m == 0),
+                stop=z == 1 and (alone or m == 2),
+            )
 
-        for m in range(2):
+        for m in range(3):
             for q in range(4):
                 one_pass(0, m, q)
-        for m, q in ((0, 0), (0, 1), (1, 0), (1, 2), (0, 2), (1, 1)):
-            one_pass(1, m, q)
-        for z in range(PASSES):
-            multiply(third_early[:], z, 2, 0, HALF, z == 0, z == 1)
-        for z in range(PASSES):
-            one_pass(z, 2, 2)
-        one_pass(0, 2, 3)
-        for m in range(3):
-            one_pass(1, m, 3)
+        for q in range(4):
+            for m in (1, 0, 2):
+                one_pass(1, m, q)
 
-        copied = keep.tile([N, 3 * QUARTER], F32, name="copied")
-        lower = keep.tile([N, 3 * QUARTER], F32, name="lower")
+        copied = keep.tile([N, S], F32, name="copied")
+        lower = keep.tile([N, S], F32, name="lower")
         lowest = keep.tile([N, S], F32, name="lowest")
 
-        def quarter(q):
-            return slice(q * QUARTER, (q + 1) * QUARTER)
-
-        for q in range(3):
-            nc.scalar.copy(out=copied[:, quarter(q)], in_=place[0, q])
-            nc.vector.tensor_tensor(lower[:, quarter(q)], place[1, q], copied[:, quarter(q)], MIN)
-        for q in range(4):
-            if q < 3:
-                nc.vector.tensor_tensor(lowest[:, quarter(q)], place[2, q], lower[:, quarter(q)], MIN)
-            else:
-                nc.vector.tensor_reduce(
-                    out=lowest[:, quarter(q)], in_=three[:].rearrange("p m s -> p s m"), axis=mybir.AxisListType.X, op=MIN
-                )
+        def reduce_and_store(q):
+            nc.vector.tensor_reduce(
+                out=lowest[:, quarter(q)], in_=trio[q][:].rearrange("p m s -> p s m"), axis=mybir.AxisListType.X, op=MIN
+            )
             nc.sync.dma_start(out=out[:, quarter(q)], in_=lowest[:, quarter(q)])
+
+        reduce_and_store(0)
+        for q in (1, 2):
+            nc.scalar.copy(out=copied[:, quarter(q)], in_=lone[q][:])
+            nc.vector.tensor_tensor(lower[:, quarter(q)], duo[q][:, 0, :], copied[:, quarter(q)], MIN)
+        for q in (1, 2):
+            nc.vector.tensor_tensor(lowest[:, quarter(q)], duo[q][:, 1, :], lower[:, quarter(q)], MIN)
+            nc.sync.dma_start(out=out[:, quarter(q)], in_=lowest[:, quarter(q)])
+        reduce_and_store(3)

@@ -53,17 +53,15 @@ def tile_picked_maxout_min_e_kernel(
         nc.gpsimd.memset(wscale[:].bitcast(I32), 0)
         for m in range(3):
             nc.sync.dma_start(
-                out=wscale[0:16, :, m * N : (m + 1) * N].bitcast(I32),
+                out=wscale[0:P:8, :, m * N : (m + 1) * N].bitcast(I32),
                 in_=w_scales[m].rearrange("z r n -> r z n").bitcast(I32),
             )
         nc.sync.dma_start(out=pairs[1][:], in_=x_rows[0, :, 2:4, :])
         nc.sync.dma_start(out=pairs[2][:], in_=x_rows[1, :, 0:2, :])
         plane2 = keep.tile([P, T], F32, name="xplane2", align_bytes=64)
         nc.sync.dma_start(out=plane2[:], in_=x_rows[1, :, 2, :])
-        for q in range(1, 4):
-            nc.sync.dma_start(
-                out=wscale[32 * q : 32 * q + 4, 0, :].bitcast(I32), in_=wscale[4 * q : 4 * q + 4, 0, :].bitcast(I32)
-            )
+        for i in range(1, 4):
+            nc.sync.dma_start(out=wscale[i:P:32].bitcast(I32), in_=wscale[8 * i : P : 32].bitcast(I32))
 
         grouped0 = keep.tile([P, S, PACK], BF16, name="grouped0", align_bytes=64)
         for j in range(PACK):
@@ -75,20 +73,20 @@ def tile_picked_maxout_min_e_kernel(
         for m in range(2):
             load_words(early_words[:, m, :], m, 0)
         nc.sync.dma_start(out=plane3[:, T // 2 : T], in_=x_rows[1, :, 3, T // 2 : T])
-        late_bytes = reuse.tile([P, 4 * PACK * N + 3 * N], U8, name="late_bytes", offset=PAIR_BYTES, align_bytes=64)
-        late_words = late_bytes[:, 0 : 4 * PACK * N].bitcast(U32).rearrange("p (a n) -> p a n", a=4)
-        wscale1 = late_bytes[:, 4 * PACK * N :]
-        nc.vector.memset(wscale1.bitcast(I32), 0)
+        late_words = reuse.tile([P, 4, N], U32, name="late_words", offset=PAIR_BYTES, align_bytes=64)
         nc.sync.dma_start(
             out=late_words[:, 0:2, :].bitcast(I32), in_=w_words[2].rearrange("z p n t -> p z (n t)").bitcast(I32)
         )
         for m in range(2):
             load_words(late_words[:, 2 + m, :], m, 1)
-        for q in range(4):
-            nc.sync.dma_start(out=wscale1[32 * q : 32 * q + 4].bitcast(I32), in_=wscale[4 * q : 4 * q + 4, 1, :].bitcast(I32))
-        w_planes = (wscale[:, 0, :], wscale1)
         words = {(0, 0): early_words[:, 0, :], (0, 1): early_words[:, 1, :], (0, 2): late_words[:, 0, :]}
         words.update({(1, 2): late_words[:, 1, :], (1, 0): late_words[:, 2, :], (1, 1): late_words[:, 3, :]})
+
+        codes0 = keep.tile([P, S], U32, name="codes0", align_bytes=64)
+        scales0 = keep.tile([P, S], U8, name="scales0", align_bytes=64)
+        nc.vector.quantize_mx(
+            out=codes0[:].bitcast(FP8X4), scales=scales0[:], in_=grouped0[:].rearrange("p s j -> p (s j)")
+        )
 
         grouped1 = [keep.tile([P, HALF, PACK], BF16, name="grouped1_%d" % h, align_bytes=64) for h in range(2)]
         picked1 = keep.tile([P, 2, S], F32, name="picked1")
@@ -98,21 +96,15 @@ def tile_picked_maxout_min_e_kernel(
             nc.scalar.copy(
                 out=grouped1[h][:, :, 0:2], in_=picked1[:, :, h * HALF : (h + 1) * HALF].rearrange("p j s -> p s j")
             )
-        late = keep.tile([P, 2, HALF], BF16, name="late", align_bytes=64)
-        nc.vector.tensor_copy(grouped1[0][:, :, 2], plane2[:].indirect(entries(0, HALF)))
-        nc.vector.tensor_copy(late[:, 0, :], plane2[:].indirect(entries(HALF, HALF)))
-
-        codes0 = keep.tile([P, S], U32, name="codes0", align_bytes=64)
-        scales0 = keep.tile([P, S], U8, name="scales0", align_bytes=64)
-        nc.vector.quantize_mx(
-            out=codes0[:].bitcast(FP8X4), scales=scales0[:], in_=grouped0[:].rearrange("p s j -> p (s j)")
-        )
-
-        nc.vector.tensor_copy(grouped1[0][:, :, 3], plane3[:].indirect(entries(0, HALF)))
-        nc.scalar.activation(late[:, 1, 0:QUARTER], plane3[:].indirect(entries(HALF, QUARTER)), COPY)
-        nc.vector.tensor_copy(late[:, 1, QUARTER:HALF], plane3[:].indirect(entries(HALF + QUARTER, QUARTER)))
+        late = keep.tile([P, 2, S], BF16, name="late", align_bytes=64)
+        nc.vector.tensor_copy(late[:, 0, :], plane2[:].indirect(offsets[:]))
         for q in range(2):
-            nc.scalar.copy(out=grouped1[1][:, quarter(q), 2:4], in_=late[:, :, quarter(q)].rearrange("p j s -> p s j"))
+            nc.vector.tensor_copy(late[:, 1, quarter(q)], plane3[:].indirect(entries(q * QUARTER, QUARTER)))
+        for q in (2, 3):
+            nc.scalar.activation(late[:, 1, quarter(q)], plane3[:].indirect(entries(q * QUARTER, QUARTER)), COPY)
+        for q in range(4):
+            lay_in = nc.vector.tensor_copy if q < 2 else nc.scalar.copy
+            lay_in(grouped1[q // 2][:, quarter(q % 2), 2:4], late[:, :, quarter(q)].rearrange("p j s -> p s j"))
 
         codes1 = keep.tile([P, S], U32, name="codes1", align_bytes=64)
         scales1 = keep.tile([P, S], U8, name="scales1", align_bytes=64)
@@ -125,49 +117,27 @@ def tile_picked_maxout_min_e_kernel(
         codes = (codes0, codes1)
         scales = (scales0, scales1)
 
-        trio = {q: psum.tile([N, 3, QUARTER], F32, name="trio%d" % q) for q in (0, 3)}
-        lone = {q: psum.tile([N, QUARTER], F32, name="lone%d" % q) for q in (1, 2)}
-        duo = {q: psum.tile([N, 2, QUARTER], F32, name="duo%d" % q) for q in (1, 2)}
-
-        def place(m, q):
-            if q in trio:
-                return trio[q][:, m, :]
-            return lone[q][:] if m == 1 else duo[q][:, m // 2, :]
+        trio = [psum.tile([N, 3, QUARTER], F32, name="trio%d" % q) for q in range(4)]
 
         def one_pass(z, m, q):
-            alone = q in lone and m == 1
             nc.tensor.matmul_mx(
-                out=place(m, q),
+                out=trio[q][:, m, :],
                 lhsT=words[z, m].bitcast(FP8X4),
-                lhsT_scale=w_planes[z][:, m * N : (m + 1) * N],
+                lhsT_scale=wscale[:, z, m * N : (m + 1) * N],
                 rhs=codes[z][:, quarter(q)].bitcast(FP8X4),
                 rhs_scale=scales[z][:, quarter(q)],
-                start=z == 0 and (alone or m == 0),
-                stop=z == 1 and (alone or m == 2),
+                start=z == 0 and m == 0,
+                stop=z == 1 and m == 2,
             )
 
         for m in range(3):
             for q in range(4):
                 one_pass(0, m, q)
+        lowest = keep.tile([N, S], F32, name="lowest")
         for q in range(4):
             for m in (1, 0, 2):
                 one_pass(1, m, q)
-
-        copied = keep.tile([N, S], F32, name="copied")
-        lower = keep.tile([N, S], F32, name="lower")
-        lowest = keep.tile([N, S], F32, name="lowest")
-
-        def reduce_and_store(q):
             nc.vector.tensor_reduce(
                 out=lowest[:, quarter(q)], in_=trio[q][:].rearrange("p m s -> p s m"), axis=mybir.AxisListType.X, op=MIN
             )
             nc.sync.dma_start(out=out[:, quarter(q)], in_=lowest[:, quarter(q)])
-
-        reduce_and_store(0)
-        for q in (1, 2):
-            nc.scalar.copy(out=copied[:, quarter(q)], in_=lone[q][:])
-            nc.vector.tensor_tensor(lower[:, quarter(q)], duo[q][:, 0, :], copied[:, quarter(q)], MIN)
-        for q in (1, 2):
-            nc.vector.tensor_tensor(lowest[:, quarter(q)], duo[q][:, 1, :], lower[:, quarter(q)], MIN)
-            nc.sync.dma_start(out=out[:, quarter(q)], in_=lowest[:, quarter(q)])
-        reduce_and_store(3)

@@ -20,6 +20,7 @@ PACK = 4
 PASSES = K // (P * PACK)
 HALF = S // 2
 QUARTER = S // 4
+EIGHTH = S // 8
 PAIR_BYTES = 2 * T * 4
 
 
@@ -67,20 +68,16 @@ def tile_picked_maxout_min_e_kernel(
         for j in range(PACK):
             nc.vector.tensor_copy(grouped0[:, :, j], pairs[j // 2][:, j % 2, :].indirect(offsets[:]))
 
+        early_words = reuse.tile([P, N], U32, name="early_words", offset=PAIR_BYTES // 2, align_bytes=64)
+        load_words(early_words[:], 0, 0)
         plane3 = reuse.tile([P, T], F32, name="xplane3", offset=0, align_bytes=64)
-        nc.sync.dma_start(out=plane3[:, 0 : T // 2], in_=x_rows[1, :, 3, 0 : T // 2])
-        early_words = reuse.tile([P, 2, N], U32, name="early_words", offset=PAIR_BYTES // 2, align_bytes=64)
-        for m in range(2):
-            load_words(early_words[:, m, :], m, 0)
-        nc.sync.dma_start(out=plane3[:, T // 2 : T], in_=x_rows[1, :, 3, T // 2 : T])
-        late_words = reuse.tile([P, 4, N], U32, name="late_words", offset=PAIR_BYTES, align_bytes=64)
-        nc.sync.dma_start(
-            out=late_words[:, 0:2, :].bitcast(I32), in_=w_words[2].rearrange("z p n t -> p z (n t)").bitcast(I32)
-        )
-        for m in range(2):
-            load_words(late_words[:, 2 + m, :], m, 1)
-        words = {(0, 0): early_words[:, 0, :], (0, 1): early_words[:, 1, :], (0, 2): late_words[:, 0, :]}
-        words.update({(1, 2): late_words[:, 1, :], (1, 0): late_words[:, 2, :], (1, 1): late_words[:, 3, :]})
+        nc.sync.dma_start(out=plane3[:], in_=x_rows[1, :, 3, :])
+        late_passes = [(z, m) for z in range(PASSES) for m in range(3)][1:]
+        late_words = reuse.tile([P, len(late_passes), N], U32, name="late_words", offset=PAIR_BYTES, align_bytes=64)
+        words = {(0, 0): early_words[:]}
+        for slot, (z, m) in enumerate(late_passes):
+            words[z, m] = late_words[:, slot, :]
+            load_words(words[z, m], m, z)
 
         codes0 = keep.tile([P, S], U32, name="codes0", align_bytes=64)
         scales0 = keep.tile([P, S], U8, name="scales0", align_bytes=64)
@@ -98,8 +95,9 @@ def tile_picked_maxout_min_e_kernel(
             )
         late = keep.tile([P, 2, S], BF16, name="late", align_bytes=64)
         nc.vector.tensor_copy(late[:, 0, :], plane2[:].indirect(offsets[:]))
-        for q in range(2):
-            nc.vector.tensor_copy(late[:, 1, quarter(q)], plane3[:].indirect(entries(q * QUARTER, QUARTER)))
+        nc.vector.tensor_copy(late[:, 1, 0:EIGHTH], plane3[:].indirect(entries(0, EIGHTH)))
+        nc.scalar.activation(late[:, 1, EIGHTH:QUARTER], plane3[:].indirect(entries(EIGHTH, EIGHTH)), COPY)
+        nc.vector.tensor_copy(late[:, 1, quarter(1)], plane3[:].indirect(entries(QUARTER, QUARTER)))
         for q in (2, 3):
             nc.scalar.activation(late[:, 1, quarter(q)], plane3[:].indirect(entries(q * QUARTER, QUARTER)), COPY)
         for q in range(4):
@@ -127,7 +125,7 @@ def tile_picked_maxout_min_e_kernel(
                 rhs=codes[z][:, quarter(q)].bitcast(FP8X4),
                 rhs_scale=scales[z][:, quarter(q)],
                 start=z == 0 and m == 0,
-                stop=z == 1 and m == 2,
+                stop=z == 1 and m == 0,
             )
 
         for m in range(3):
@@ -135,7 +133,7 @@ def tile_picked_maxout_min_e_kernel(
                 one_pass(0, m, q)
         lowest = keep.tile([N, S], F32, name="lowest")
         for q in range(4):
-            for m in (1, 0, 2):
+            for m in (2, 1, 0):
                 one_pass(1, m, q)
             nc.vector.tensor_reduce(
                 out=lowest[:, quarter(q)], in_=trio[q][:].rearrange("p m s -> p s m"), axis=mybir.AxisListType.X, op=MIN

@@ -68,15 +68,11 @@ def tile_picked_maxout_min_e_kernel(
         for j in range(PACK):
             nc.vector.tensor_copy(grouped0[:, :, j], pairs[j // 2][:, j % 2, :].indirect(offsets[:]))
 
-        early_words = reuse.tile([P, N], U32, name="early_words", offset=PAIR_BYTES // 2, align_bytes=64)
-        load_words(early_words[:], 0, 0)
         plane3 = reuse.tile([P, T], F32, name="xplane3", offset=0, align_bytes=64)
         nc.sync.dma_start(out=plane3[:], in_=x_rows[1, :, 3, :])
-        late_passes = [(z, m) for z in range(PASSES) for m in range(3)][1:]
-        late_words = reuse.tile([P, len(late_passes), N], U32, name="late_words", offset=PAIR_BYTES, align_bytes=64)
-        words = {(0, 0): early_words[:]}
-        for slot, (z, m) in enumerate(late_passes):
-            words[z, m] = late_words[:, slot, :]
+        all_words = reuse.tile([P, PASSES, 3, N], U32, name="all_words", offset=PAIR_BYTES, align_bytes=64)
+        words = {(z, m): all_words[:, z, m, :] for z in range(PASSES) for m in range(3)}
+        for z, m in words:
             load_words(words[z, m], m, z)
 
         codes0 = keep.tile([P, S], U32, name="codes0", align_bytes=64)
@@ -117,24 +113,28 @@ def tile_picked_maxout_min_e_kernel(
 
         trio = [psum.tile([N, 3, QUARTER], F32, name="trio%d" % q) for q in range(4)]
 
-        def one_pass(z, m, q):
+        def one_pass(z, m, q, start, stop):
             nc.tensor.matmul_mx(
                 out=trio[q][:, m, :],
                 lhsT=words[z, m].bitcast(FP8X4),
                 lhsT_scale=wscale[:, z, m * N : (m + 1) * N],
                 rhs=codes[z][:, quarter(q)].bitcast(FP8X4),
                 rhs_scale=scales[z][:, quarter(q)],
-                start=z == 0 and m == 0,
-                stop=z == 1 and m == 0,
+                start=start,
+                stop=stop,
             )
 
         for m in range(3):
-            for q in range(4):
-                one_pass(0, m, q)
+            for q in range(3):
+                one_pass(0, m, q, m == 0, False)
         lowest = keep.tile([N, S], F32, name="lowest")
         for q in range(4):
+            last = q == 3
             for m in (2, 1, 0):
-                one_pass(1, m, q)
+                one_pass(1, m, q, last and m == 2, m == 0 and not last)
+            if last:
+                for m in range(3):
+                    one_pass(0, m, q, False, m == 2)
             nc.vector.tensor_reduce(
                 out=lowest[:, quarter(q)], in_=trio[q][:].rearrange("p m s -> p s m"), axis=mybir.AxisListType.X, op=MIN
             )

@@ -46,27 +46,33 @@ def tile_picked_maxout_min_e_kernel(
         def load_words(dst, m, z):
             nc.sync.dma_start(out=dst.bitcast(I32), in_=w_words[m][z].rearrange("p n t -> p (n t)").bitcast(I32))
 
-        pairs = [reuse.tile([P, 2, T], F32, name="xpair%d" % u, offset=u * PAIR_BYTES, align_bytes=64) for u in range(3)]
+        first = reuse.tile([P, PACK, T], F32, name="xfirst", offset=0, align_bytes=64)
         offsets = keep.tile([P, S // 16], U16, name="offsets")
-        nc.sync.dma_start(out=pairs[0][:], in_=x_rows[0, :, 0:2, :])
+        nc.sync.dma_start(out=first[:], in_=x_rows[0])
         nc.sync.dma_start(offsets[:], offs)
         wscale = keep.tile([P, PASSES, 3 * N], U8, name="wscale", align_bytes=64)
-        nc.gpsimd.memset(wscale[:].bitcast(I32), 0)
+        nc.gpsimd.memset(wscale[:, 0, :].bitcast(I32), 0)
+        nc.scalar.copy(out=wscale[:, 1, :].bitcast(U32), in_=wscale[:, 0, :].bitcast(U32))
         for m in range(3):
             nc.sync.dma_start(
                 out=wscale[0:P:8, :, m * N : (m + 1) * N].bitcast(I32),
                 in_=w_scales[m].rearrange("z r n -> r z n").bitcast(I32),
             )
-        nc.sync.dma_start(out=pairs[1][:], in_=x_rows[0, :, 2:4, :])
-        nc.sync.dma_start(out=pairs[2][:], in_=x_rows[1, :, 0:2, :])
+        pair = keep.tile([P, 2, T], F32, name="xpair", align_bytes=64)
+        nc.sync.dma_start(out=pair[:], in_=x_rows[1, :, 0:2, :])
         plane2 = keep.tile([P, T], F32, name="xplane2", align_bytes=64)
         nc.sync.dma_start(out=plane2[:], in_=x_rows[1, :, 2, :])
         for i in range(1, 4):
             nc.sync.dma_start(out=wscale[i:P:32].bitcast(I32), in_=wscale[8 * i : P : 32].bitcast(I32))
 
         grouped0 = keep.tile([P, S, PACK], BF16, name="grouped0", align_bytes=64)
-        for j in range(PACK):
-            nc.vector.tensor_copy(grouped0[:, :, j], pairs[j // 2][:, j % 2, :].indirect(offsets[:]))
+        picked0 = keep.tile([P, 2, S], F32, name="picked0")
+        nc.vector.tensor_copy(picked0[:, 1, 0:HALF], first[:, 1, :].indirect(entries(0, HALF)))
+        nc.scalar.activation(picked0[:, 0, :], first[:, 0, :].indirect(offsets[:]), COPY)
+        nc.scalar.activation(picked0[:, 1, HALF:S], first[:, 1, :].indirect(entries(HALF, HALF)), COPY)
+        for j in (2, 3):
+            nc.vector.tensor_copy(grouped0[:, :, j], first[:, j, :].indirect(offsets[:]))
+        nc.scalar.copy(out=grouped0[:, :, 0:2], in_=picked0[:].rearrange("p j s -> p s j"))
 
         plane3 = reuse.tile([P, T], F32, name="xplane3", offset=0, align_bytes=64)
         nc.sync.dma_start(out=plane3[:], in_=x_rows[1, :, 3, :])
@@ -83,14 +89,17 @@ def tile_picked_maxout_min_e_kernel(
 
         grouped1 = [keep.tile([P, HALF, PACK], BF16, name="grouped1_%d" % h, align_bytes=64) for h in range(2)]
         picked1 = keep.tile([P, 2, S], F32, name="picked1")
-        for e in range(2):
-            nc.vector.tensor_copy(picked1[:, e, :], pairs[2][:, e, :].indirect(offsets[:]))
         for h in range(2):
+            for e in range(2):
+                nc.vector.tensor_copy(
+                    picked1[:, e, h * HALF : (h + 1) * HALF], pair[:, e, :].indirect(entries(h * HALF, HALF))
+                )
             nc.scalar.copy(
                 out=grouped1[h][:, :, 0:2], in_=picked1[:, :, h * HALF : (h + 1) * HALF].rearrange("p j s -> p s j")
             )
         late = keep.tile([P, 2, S], BF16, name="late", align_bytes=64)
-        nc.vector.tensor_copy(late[:, 0, :], plane2[:].indirect(offsets[:]))
+        nc.vector.tensor_copy(late[:, 0, 0 : S - QUARTER], plane2[:].indirect(entries(0, S - QUARTER)))
+        nc.scalar.activation(late[:, 0, quarter(3)], plane2[:].indirect(entries(S - QUARTER, QUARTER)), COPY)
         nc.vector.tensor_copy(late[:, 1, 0:EIGHTH], plane3[:].indirect(entries(0, EIGHTH)))
         nc.scalar.activation(late[:, 1, EIGHTH:QUARTER], plane3[:].indirect(entries(EIGHTH, EIGHTH)), COPY)
         nc.vector.tensor_copy(late[:, 1, quarter(1)], plane3[:].indirect(entries(QUARTER, QUARTER)))

@@ -20,7 +20,7 @@ PACK = 4
 PASSES = K // (P * PACK)
 HALF = S // 2
 QUARTER = S // 4
-EIGHTH = S // 8
+WARM_M = 32
 PAIR_BYTES = 2 * T * 4
 
 
@@ -58,7 +58,7 @@ def tile_picked_maxout_min_e_kernel(
                 out=wscale[0:P:8, :, m * N : (m + 1) * N].bitcast(I32),
                 in_=w_scales[m].rearrange("z r n -> r z n").bitcast(I32),
             )
-        pair = keep.tile([P, 2, T], F32, name="xpair", align_bytes=64)
+        pair = reuse.tile([P, 2, T], F32, name="xpair", offset=2 * PAIR_BYTES, align_bytes=64)
         nc.sync.dma_start(out=pair[:], in_=x_rows[1, :, 0:2, :])
         plane2 = keep.tile([P, T], F32, name="xplane2", align_bytes=64)
         nc.sync.dma_start(out=plane2[:], in_=x_rows[1, :, 2, :])
@@ -82,10 +82,14 @@ def tile_picked_maxout_min_e_kernel(
             load_words(words[z, m], m, z)
 
         codes0 = keep.tile([P, S], U32, name="codes0", align_bytes=64)
-        scales0 = keep.tile([P, S], U8, name="scales0", align_bytes=64)
-        nc.vector.quantize_mx(
-            out=codes0[:].bitcast(FP8X4), scales=scales0[:], in_=grouped0[:].rearrange("p s j -> p (s j)")
-        )
+        scales0 = keep.tile([P, S - QUARTER], U8, name="scales0", align_bytes=64)
+
+        def quantise(codes_out, scales_out, grouped):
+            nc.vector.quantize_mx(
+                out=codes_out.bitcast(FP8X4), scales=scales_out, in_=grouped.rearrange("p s j -> p (s j)")
+            )
+
+        quantise(codes0[:, 0 : S - QUARTER], scales0[:], grouped0[:, 0 : S - QUARTER, :])
 
         grouped1 = [keep.tile([P, HALF, PACK], BF16, name="grouped1_%d" % h, align_bytes=64) for h in range(2)]
         picked1 = keep.tile([P, 2, S], F32, name="picked1")
@@ -97,28 +101,26 @@ def tile_picked_maxout_min_e_kernel(
             nc.scalar.copy(
                 out=grouped1[h][:, :, 0:2], in_=picked1[:, :, h * HALF : (h + 1) * HALF].rearrange("p j s -> p s j")
             )
-        late = keep.tile([P, 2, S], BF16, name="late", align_bytes=64)
-        nc.vector.tensor_copy(late[:, 0, 0 : S - QUARTER], plane2[:].indirect(entries(0, S - QUARTER)))
-        nc.scalar.activation(late[:, 0, quarter(3)], plane2[:].indirect(entries(S - QUARTER, QUARTER)), COPY)
-        nc.vector.tensor_copy(late[:, 1, 0:EIGHTH], plane3[:].indirect(entries(0, EIGHTH)))
-        nc.scalar.activation(late[:, 1, EIGHTH:QUARTER], plane3[:].indirect(entries(EIGHTH, EIGHTH)), COPY)
-        nc.vector.tensor_copy(late[:, 1, quarter(1)], plane3[:].indirect(entries(QUARTER, QUARTER)))
-        for q in (2, 3):
-            nc.scalar.activation(late[:, 1, quarter(q)], plane3[:].indirect(entries(q * QUARTER, QUARTER)), COPY)
-        for q in range(4):
-            lay_in = nc.vector.tensor_copy if q < 2 else nc.scalar.copy
-            lay_in(grouped1[q // 2][:, quarter(q % 2), 2:4], late[:, :, quarter(q)].rearrange("p j s -> p s j"))
+        scales0_last = reuse.tile([P, QUARTER], U8, name="scales0_last", offset=2 * PAIR_BYTES, align_bytes=64)
+        quantise(codes0[:, quarter(3)], scales0_last[:], grouped0[:, quarter(3), :])
+        late = keep.tile([P, 2, HALF], BF16, name="late", align_bytes=64)
+        nc.vector.tensor_copy(grouped1[0][:, :, 2], plane2[:].indirect(entries(0, HALF)))
+        nc.vector.tensor_copy(late[:, 0, quarter(0)], plane2[:].indirect(entries(HALF, QUARTER)))
+        nc.scalar.activation(late[:, 0, quarter(1)], plane2[:].indirect(entries(HALF + QUARTER, QUARTER)), COPY)
+        nc.vector.tensor_copy(grouped1[0][:, :, 3], plane3[:].indirect(entries(0, HALF)))
+        for q in range(2):
+            nc.scalar.activation(late[:, 1, quarter(q)], plane3[:].indirect(entries(HALF + q * QUARTER, QUARTER)), COPY)
+        for q in range(2):
+            nc.scalar.copy(out=grouped1[1][:, quarter(q), 2:4], in_=late[:, :, quarter(q)].rearrange("p j s -> p s j"))
 
         codes1 = keep.tile([P, S], U32, name="codes1", align_bytes=64)
         scales1 = keep.tile([P, S], U8, name="scales1", align_bytes=64)
         for q in range(4):
-            nc.vector.quantize_mx(
-                out=codes1[:, quarter(q)].bitcast(FP8X4),
-                scales=scales1[:, quarter(q)],
-                in_=grouped1[q // 2][:, quarter(q % 2), :].rearrange("p s j -> p (s j)"),
-            )
+            quantise(codes1[:, quarter(q)], scales1[:, quarter(q)], grouped1[q // 2][:, quarter(q % 2), :])
         codes = (codes0, codes1)
-        scales = (scales0, scales1)
+        planes = {(1, q): scales1[:, quarter(q)] for q in range(4)}
+        planes.update({(0, q): scales0[:, quarter(q)] for q in range(3)})
+        planes[0, 3] = scales0_last[:]
 
         trio = [psum.tile([N, 3, QUARTER], F32, name="trio%d" % q) for q in range(4)]
 
@@ -128,9 +130,21 @@ def tile_picked_maxout_min_e_kernel(
                 lhsT=words[z, m].bitcast(FP8X4),
                 lhsT_scale=wscale[:, z, m * N : (m + 1) * N],
                 rhs=codes[z][:, quarter(q)].bitcast(FP8X4),
-                rhs_scale=scales[z][:, quarter(q)],
+                rhs_scale=planes[z, q],
                 start=start,
                 stop=stop,
+            )
+
+        idle = psum.tile([WARM_M, S], F32, name="idle")
+        for width in (S, S, QUARTER):
+            nc.tensor.matmul_mx(
+                out=idle[:, 0:width],
+                lhsT=codes0[:, 0:WARM_M].bitcast(FP8X4),
+                lhsT_scale=scales0[:, 0:WARM_M],
+                rhs=codes0[:, S - width : S].bitcast(FP8X4),
+                rhs_scale=wscale[:].rearrange("p z n -> p (z n)")[:, 0:width],
+                start=True,
+                stop=True,
             )
 
         for m in range(3):

@@ -62,8 +62,6 @@ def tile_picked_maxout_min_e_kernel(
         nc.sync.dma_start(out=pair[:], in_=x_rows[1, :, 0:2, :])
         plane2 = keep.tile([P, T], F32, name="xplane2", align_bytes=64)
         nc.sync.dma_start(out=plane2[:], in_=x_rows[1, :, 2, :])
-        for i in range(1, 4):
-            nc.sync.dma_start(out=wscale[i:P:32].bitcast(I32), in_=wscale[8 * i : P : 32].bitcast(I32))
 
         grouped0 = keep.tile([P, S, PACK], BF16, name="grouped0", align_bytes=64)
         picked0 = keep.tile([P, 2, S], F32, name="picked0")
@@ -76,10 +74,10 @@ def tile_picked_maxout_min_e_kernel(
 
         plane3 = reuse.tile([P, T], F32, name="xplane3", offset=0, align_bytes=64)
         nc.sync.dma_start(out=plane3[:], in_=x_rows[1, :, 3, :])
-        all_words = reuse.tile([P, PASSES, 3, N], U32, name="all_words", offset=PAIR_BYTES, align_bytes=64)
-        words = {(z, m): all_words[:, z, m, :] for z in range(PASSES) for m in range(3)}
-        for z, m in words:
-            load_words(words[z, m], m, z)
+        placed = reuse.tile([P, PASSES, 3 * N], U8, name="placed", offset=PAIR_BYTES, align_bytes=64)
+        nc.gpsimd.tensor_copy(placed[:].bitcast(I32), wscale[:].bitcast(I32))
+        for i in range(1, 4):
+            nc.sync.dma_start(out=placed[i:P:32].bitcast(I32), in_=wscale[8 * i : P : 32].bitcast(I32))
 
         codes0 = keep.tile([P, S], U32, name="codes0", align_bytes=64)
         scales0 = keep.tile([P, S - QUARTER], U8, name="scales0", align_bytes=64)
@@ -92,21 +90,25 @@ def tile_picked_maxout_min_e_kernel(
         quantise(codes0[:, 0 : S - QUARTER], scales0[:], grouped0[:, 0 : S - QUARTER, :])
 
         grouped1 = [keep.tile([P, HALF, PACK], BF16, name="grouped1_%d" % h, align_bytes=64) for h in range(2)]
-        picked1 = keep.tile([P, 2, S], F32, name="picked1")
-        for h in range(2):
-            for e in range(2):
-                nc.vector.tensor_copy(
-                    picked1[:, e, h * HALF : (h + 1) * HALF], pair[:, e, :].indirect(entries(h * HALF, HALF))
-                )
-            nc.scalar.copy(
-                out=grouped1[h][:, :, 0:2], in_=picked1[:, :, h * HALF : (h + 1) * HALF].rearrange("p j s -> p s j")
-            )
+        picked1 = keep.tile([P, 2, HALF], F32, name="picked1")
+        nc.vector.tensor_copy(picked1[:, 1, :], pair[:, 1, :].indirect(entries(HALF, HALF)))
+        nc.scalar.activation(picked1[:, 0, :], pair[:, 0, :].indirect(entries(HALF, HALF)), COPY)
+        for j in range(2):
+            nc.vector.tensor_copy(grouped1[0][:, :, j], pair[:, j, :].indirect(entries(0, HALF)))
+        nc.scalar.copy(out=grouped1[1][:, :, 0:2], in_=picked1[:].rearrange("p j s -> p s j"))
         scales0_last = reuse.tile([P, QUARTER], U8, name="scales0_last", offset=2 * PAIR_BYTES, align_bytes=64)
         quantise(codes0[:, quarter(3)], scales0_last[:], grouped0[:, quarter(3), :])
+        all_words = reuse.tile([P, 3, PASSES, N], U32, name="all_words", offset=5 * PAIR_BYTES // 2, align_bytes=64)
+        words = {(z, m): all_words[:, m, z, :] for z in range(PASSES) for m in range(3)}
+        load_words(words[0, 0], 0, 0)
+        for m in (1, 2):
+            nc.sync.dma_start(
+                out=all_words[:, m, :, :].bitcast(I32), in_=w_words[m].rearrange("z p n t -> p z (n t)").bitcast(I32)
+            )
+        load_words(words[1, 0], 0, 1)
         late = keep.tile([P, 2, HALF], BF16, name="late", align_bytes=64)
         nc.vector.tensor_copy(grouped1[0][:, :, 2], plane2[:].indirect(entries(0, HALF)))
-        nc.vector.tensor_copy(late[:, 0, quarter(0)], plane2[:].indirect(entries(HALF, QUARTER)))
-        nc.scalar.activation(late[:, 0, quarter(1)], plane2[:].indirect(entries(HALF + QUARTER, QUARTER)), COPY)
+        nc.scalar.activation(late[:, 0, :], plane2[:].indirect(entries(HALF, HALF)), COPY)
         nc.vector.tensor_copy(grouped1[0][:, :, 3], plane3[:].indirect(entries(0, HALF)))
         for q in range(2):
             nc.scalar.activation(late[:, 1, quarter(q)], plane3[:].indirect(entries(HALF + q * QUARTER, QUARTER)), COPY)
@@ -128,7 +130,7 @@ def tile_picked_maxout_min_e_kernel(
             nc.tensor.matmul_mx(
                 out=trio[q][:, m, :],
                 lhsT=words[z, m].bitcast(FP8X4),
-                lhsT_scale=wscale[:, z, m * N : (m + 1) * N],
+                lhsT_scale=placed[:, z, m * N : (m + 1) * N],
                 rhs=codes[z][:, quarter(q)].bitcast(FP8X4),
                 rhs_scale=planes[z, q],
                 start=start,
@@ -147,17 +149,14 @@ def tile_picked_maxout_min_e_kernel(
                 stop=True,
             )
 
-        for m in range(3):
-            for q in range(3):
-                one_pass(0, m, q, m == 0, False)
+        early = [(m, q) for m in range(3) for q in range(3)][:-1]
+        for m, q in early:
+            one_pass(0, m, q, m == 0, False)
         lowest = keep.tile([N, S], F32, name="lowest")
         for q in range(4):
-            last = q == 3
-            for m in (2, 1, 0):
-                one_pass(1, m, q, last and m == 2, m == 0 and not last)
-            if last:
-                for m in range(3):
-                    one_pass(0, m, q, False, m == 2)
+            late_passes = [(1, m) for m in range(3)] + [(0, m) for m in range(3) if (m, q) not in early]
+            for z, m in late_passes:
+                one_pass(z, m, q, q == 3 and (z, m) == late_passes[0], (z, m) == late_passes[-1])
             nc.vector.tensor_reduce(
                 out=lowest[:, quarter(q)], in_=trio[q][:].rearrange("p m s -> p s m"), axis=mybir.AxisListType.X, op=MIN
             )

@@ -149,12 +149,14 @@ def tile_picked_maxout_min_e_kernel(
                 stop=True,
             )
 
-        early = [(m, q) for m in range(3) for q in range(3)][:-1]
+        early = [(m, q) for m in range(2) for q in range(3)] + [(2, 0)]
         for m, q in early:
             one_pass(0, m, q, m == 0, False)
         lowest = keep.tile([N, S], F32, name="lowest")
         for q in range(4):
             late_passes = [(1, m) for m in range(3)] + [(0, m) for m in range(3) if (m, q) not in early]
+            if q == 0:
+                late_passes.reverse()
             for z, m in late_passes:
                 one_pass(z, m, q, q == 3 and (z, m) == late_passes[0], (z, m) == late_passes[-1])
             nc.vector.tensor_reduce(

@@ -75,7 +75,7 @@ def tile_picked_maxout_min_e_kernel(
         plane3 = reuse.tile([P, T], F32, name="xplane3", offset=0, align_bytes=64)
         nc.sync.dma_start(out=plane3[:], in_=x_rows[1, :, 3, :])
         placed = reuse.tile([P, PASSES, 3 * N], U8, name="placed", offset=PAIR_BYTES, align_bytes=64)
-        nc.gpsimd.tensor_copy(placed[:].bitcast(I32), wscale[:].bitcast(I32))
+        nc.scalar.copy(out=placed[:].bitcast(U32), in_=wscale[:].bitcast(U32))
         for i in range(1, 4):
             nc.sync.dma_start(out=placed[i:P:32].bitcast(I32), in_=wscale[8 * i : P : 32].bitcast(I32))
 

@@ -91,8 +91,8 @@ def tile_picked_maxout_min_e_kernel(
 
         grouped1 = [keep.tile([P, HALF, PACK], BF16, name="grouped1_%d" % h, align_bytes=64) for h in range(2)]
         picked1 = keep.tile([P, 2, HALF], F32, name="picked1")
-        nc.vector.tensor_copy(picked1[:, 1, :], pair[:, 1, :].indirect(entries(HALF, HALF)))
-        nc.scalar.activation(picked1[:, 0, :], pair[:, 0, :].indirect(entries(HALF, HALF)), COPY)
+        for j in range(2):
+            nc.scalar.activation(picked1[:, j, :], pair[:, j, :].indirect(entries(HALF, HALF)), COPY)
         for j in range(2):
             nc.vector.tensor_copy(grouped1[0][:, :, j], pair[:, j, :].indirect(entries(0, HALF)))
         nc.scalar.copy(out=grouped1[1][:, :, 0:2], in_=picked1[:].rearrange("p j s -> p s j"))

@@ -58,6 +58,10 @@ def tile_picked_maxout_min_e_kernel(
                 out=wscale[0:P:8, :, m * N : (m + 1) * N].bitcast(I32),
                 in_=w_scales[m].rearrange("z r n -> r z n").bitcast(I32),
             )
+        placed = keep.tile([P, PASSES, 3 * N], U8, name="placed", align_bytes=64)
+        nc.scalar.copy(out=placed[:].bitcast(U32), in_=wscale[:].bitcast(U32))
+        for i in range(1, 4):
+            nc.gpsimd.dma_start(out=placed[i:P:32].bitcast(I32), in_=wscale[8 * i : P : 32].bitcast(I32))
         pair = reuse.tile([P, 2, T], F32, name="xpair", offset=2 * PAIR_BYTES, align_bytes=64)
         nc.sync.dma_start(out=pair[:], in_=x_rows[1, :, 0:2, :])
         plane2 = keep.tile([P, T], F32, name="xplane2", align_bytes=64)
@@ -74,10 +78,6 @@ def tile_picked_maxout_min_e_kernel(
 
         plane3 = reuse.tile([P, T], F32, name="xplane3", offset=0, align_bytes=64)
         nc.sync.dma_start(out=plane3[:], in_=x_rows[1, :, 3, :])
-        placed = reuse.tile([P, PASSES, 3 * N], U8, name="placed", offset=PAIR_BYTES, align_bytes=64)
-        nc.scalar.copy(out=placed[:].bitcast(U32), in_=wscale[:].bitcast(U32))
-        for i in range(1, 4):
-            nc.sync.dma_start(out=placed[i:P:32].bitcast(I32), in_=wscale[8 * i : P : 32].bitcast(I32))
 
         codes0 = keep.tile([P, S], U32, name="codes0", align_bytes=64)
         scales0 = keep.tile([P, S - QUARTER], U8, name="scales0", align_bytes=64)

@@ -106,7 +106,7 @@ def tile_picked_maxout_min_e_kernel(
                 out=all_words[:, m, :, :].bitcast(I32), in_=w_words[m].rearrange("z p n t -> p z (n t)").bitcast(I32)
             )
         load_words(words[1, 0], 0, 1)
-        late = keep.tile([P, 2, HALF], BF16, name="late", align_bytes=64)
+        late = reuse.tile([P, 2, HALF], BF16, name="late", offset=3 * PAIR_BYTES, align_bytes=64)
         nc.vector.tensor_copy(grouped1[0][:, :, 2], plane2[:].indirect(entries(0, HALF)))
         nc.scalar.activation(late[:, 0, :], plane2[:].indirect(entries(HALF, HALF)), COPY)
         nc.vector.tensor_copy(grouped1[0][:, :, 3], plane3[:].indirect(entries(0, HALF)))
@@ -124,11 +124,15 @@ def tile_picked_maxout_min_e_kernel(
         planes.update({(0, q): scales0[:, quarter(q)] for q in range(3)})
         planes[0, 3] = scales0_last[:]
 
-        trio = [psum.tile([N, 3, QUARTER], F32, name="trio%d" % q) for q in range(4)]
+        duo = psum.tile([N, 2, QUARTER], F32, name="duo")
+        solo = psum.tile([N, QUARTER], F32, name="solo")
+        trio = {q: psum.tile([N, 3, QUARTER], F32, name="trio%d" % q) for q in range(1, 4)}
+        sums = {(m, q): trio[q][:, m, :] for m in range(3) for q in range(1, 4)}
+        sums.update({(0, 0): solo[:], (1, 0): duo[:, 0, :], (2, 0): duo[:, 1, :]})
 
         def one_pass(z, m, q, start, stop):
             nc.tensor.matmul_mx(
-                out=trio[q][:, m, :],
+                out=sums[m, q],
                 lhsT=words[z, m].bitcast(FP8X4),
                 lhsT_scale=placed[:, z, m * N : (m + 1) * N],
                 rhs=codes[z][:, quarter(q)].bitcast(FP8X4),
@@ -149,17 +153,33 @@ def tile_picked_maxout_min_e_kernel(
                 stop=True,
             )
 
-        early = [(m, q) for m in range(2) for q in range(3)] + [(2, 0)]
-        for m, q in early:
-            one_pass(0, m, q, m == 0, False)
+        for m in range(2):
+            for q in range(3):
+                one_pass(0, m, q, m == 0 or q == 0, False)
+        for q in range(2):
+            one_pass(0, 2, q, False, False)
+        for q in range(2):
+            for m in (1, 2):
+                one_pass(1, m, q, False, (m, q) == (2, 0))
         lowest = keep.tile([N, S], F32, name="lowest")
-        for q in range(4):
-            late_passes = [(1, m) for m in range(3)] + [(0, m) for m in range(3) if (m, q) not in early]
-            if q == 0:
-                late_passes.reverse()
+        partial = reuse.tile([N, QUARTER], F32, name="partial", offset=3 * PAIR_BYTES, align_bytes=64)
+
+        def smallest(dst, bank):
+            nc.vector.tensor_reduce(out=dst, in_=bank.rearrange("p m s -> p s m"), axis=mybir.AxisListType.X, op=MIN)
+
+        def store(q):
+            nc.sync.dma_start(out=out[:, quarter(q)], in_=lowest[:, quarter(q)])
+
+        smallest(partial[:], duo[:])
+        one_pass(1, 0, 1, False, True)
+        one_pass(1, 0, 0, False, True)
+        smallest(lowest[:, quarter(1)], trio[1][:])
+        store(1)
+        nc.vector.tensor_tensor(lowest[:, quarter(0)], solo[:], partial[:], MIN)
+        store(0)
+        for q in (2, 3):
+            late_passes = [(1, m) for m in range(3)] + [(0, m) for m in range(3) if q == 3 or m == 2]
             for z, m in late_passes:
                 one_pass(z, m, q, q == 3 and (z, m) == late_passes[0], (z, m) == late_passes[-1])
-            nc.vector.tensor_reduce(
-                out=lowest[:, quarter(q)], in_=trio[q][:].rearrange("p m s -> p s m"), axis=mybir.AxisListType.X, op=MIN
-            )
-            nc.sync.dma_start(out=out[:, quarter(q)], in_=lowest[:, quarter(q)])
+            smallest(lowest[:, quarter(q)], trio[q][:])
+            store(q)

from contextlib import ExitStack

import concourse.mybir as mybir

K, T, S, N = 1024, 2048, 512, 128
FLOPS = 3 * 2 * K * S * N

F32 = mybir.dt.float32
BF16 = mybir.dt.bfloat16
I32 = mybir.dt.int32
U32 = mybir.dt.uint32
U16 = mybir.dt.uint16
U8 = mybir.dt.uint8
FP8X4 = mybir.dt.float8_e4m3fn_x4
MIN = mybir.AluOpType.min
COPY = mybir.ActivationFunctionType.Copy

P = 128
PACK = 4
PASSES = K // (P * PACK)
HALF = S // 2
QUARTER = S // 4
WARM_M = 32
PAIR_BYTES = 2 * T * 4


def tile_picked_maxout_min_e_kernel(
    tc, xT, w1_words, w1_scales, w2_words, w2_scales, w3_words, w3_scales, offs, out
):
    nc = tc.nc
    w_words = (w1_words, w2_words, w3_words)
    w_scales = (w1_scales, w2_scales, w3_scales)
    x_rows = xT.rearrange("(z p j) t -> z p j t", z=PASSES, j=PACK)

    with ExitStack() as ctx:
        keep = ctx.enter_context(tc.tile_pool(name="keep", bufs=1))
        reuse = ctx.enter_context(tc.tile_pool(name="reuse", bufs=1))
        psum = ctx.enter_context(tc.psum_pool(name="psum", bufs=1))

        def entries(first, count):
            return offsets[:, first // 16 : (first + count) // 16]

        def quarter(q):
            return slice(q * QUARTER, (q + 1) * QUARTER)

        def load_words(dst, m, z):
            nc.sync.dma_start(out=dst.bitcast(I32), in_=w_words[m][z].rearrange("p n t -> p (n t)").bitcast(I32))

        first = reuse.tile([P, PACK, T], F32, name="xfirst", offset=0, align_bytes=64)
        offsets = keep.tile([P, S // 16], U16, name="offsets")
        nc.sync.dma_start(out=first[:], in_=x_rows[0])
        nc.sync.dma_start(offsets[:], offs)
        wscale = keep.tile([P, PASSES, 3 * N], U8, name="wscale", align_bytes=64)
        nc.gpsimd.memset(wscale[:, 0, :].bitcast(I32), 0)
        nc.scalar.copy(out=wscale[:, 1, :].bitcast(U32), in_=wscale[:, 0, :].bitcast(U32))
        for m in range(3):
            nc.sync.dma_start(
                out=wscale[0:P:8, :, m * N : (m + 1) * N].bitcast(I32),
                in_=w_scales[m].rearrange("z r n -> r z n").bitcast(I32),
            )
        placed = keep.tile([P, PASSES, 3 * N], U8, name="placed", align_bytes=64)
        nc.scalar.copy(out=placed[:].bitcast(U32), in_=wscale[:].bitcast(U32))
        for i in range(1, 4):
            nc.gpsimd.dma_start(out=placed[i:P:32].bitcast(I32), in_=wscale[8 * i : P : 32].bitcast(I32))
        pair = reuse.tile([P, 2, T], F32, name="xpair", offset=2 * PAIR_BYTES, align_bytes=64)
        nc.sync.dma_start(out=pair[:], in_=x_rows[1, :, 0:2, :])
        plane2 = keep.tile([P, T], F32, name="xplane2", align_bytes=64)
        nc.sync.dma_start(out=plane2[:], in_=x_rows[1, :, 2, :])

        grouped0 = keep.tile([P, S, PACK], BF16, name="grouped0", align_bytes=64)
        picked0 = keep.tile([P, 2, S], F32, name="picked0")
        nc.vector.tensor_copy(picked0[:, 1, 0:HALF], first[:, 1, :].indirect(entries(0, HALF)))
        nc.scalar.activation(picked0[:, 0, :], first[:, 0, :].indirect(offsets[:]), COPY)
        nc.scalar.activation(picked0[:, 1, HALF:S], first[:, 1, :].indirect(entries(HALF, HALF)), COPY)
        for j in (2, 3):
            nc.vector.tensor_copy(grouped0[:, :, j], first[:, j, :].indirect(offsets[:]))
        nc.scalar.copy(out=grouped0[:, :, 0:2], in_=picked0[:].rearrange("p j s -> p s j"))

        plane3 = reuse.tile([P, T], F32, name="xplane3", offset=0, align_bytes=64)
        nc.sync.dma_start(out=plane3[:], in_=x_rows[1, :, 3, :])

        codes0 = keep.tile([P, S], U32, name="codes0", align_bytes=64)
        scales0 = keep.tile([P, S - QUARTER], U8, name="scales0", align_bytes=64)

        def quantise(codes_out, scales_out, grouped):
            nc.vector.quantize_mx(
                out=codes_out.bitcast(FP8X4), scales=scales_out, in_=grouped.rearrange("p s j -> p (s j)")
            )

        quantise(codes0[:, 0 : S - QUARTER], scales0[:], grouped0[:, 0 : S - QUARTER, :])

        grouped1 = [keep.tile([P, HALF, PACK], BF16, name="grouped1_%d" % h, align_bytes=64) for h in range(2)]
        picked1 = keep.tile([P, 2, HALF], F32, name="picked1")
        for j in range(2):
            nc.scalar.activation(picked1[:, j, :], pair[:, j, :].indirect(entries(HALF, HALF)), COPY)
        for j in range(2):
            nc.vector.tensor_copy(grouped1[0][:, :, j], pair[:, j, :].indirect(entries(0, HALF)))
        nc.scalar.copy(out=grouped1[1][:, :, 0:2], in_=picked1[:].rearrange("p j s -> p s j"))
        scales0_last = reuse.tile([P, QUARTER], U8, name="scales0_last", offset=2 * PAIR_BYTES, align_bytes=64)
        quantise(codes0[:, quarter(3)], scales0_last[:], grouped0[:, quarter(3), :])
        all_words = reuse.tile([P, 3, PASSES, N], U32, name="all_words", offset=5 * PAIR_BYTES // 2, align_bytes=64)
        words = {(z, m): all_words[:, m, z, :] for z in range(PASSES) for m in range(3)}
        load_words(words[0, 0], 0, 0)
        for m in (1, 2):
            nc.sync.dma_start(
                out=all_words[:, m, :, :].bitcast(I32), in_=w_words[m].rearrange("z p n t -> p z (n t)").bitcast(I32)
            )
        load_words(words[1, 0], 0, 1)
        late = reuse.tile([P, 2, HALF], BF16, name="late", offset=3 * PAIR_BYTES, align_bytes=64)
        nc.vector.tensor_copy(grouped1[0][:, :, 2], plane2[:].indirect(entries(0, HALF)))
        nc.scalar.activation(late[:, 0, :], plane2[:].indirect(entries(HALF, HALF)), COPY)
        nc.vector.tensor_copy(grouped1[0][:, :, 3], plane3[:].indirect(entries(0, HALF)))
        for q in range(2):
            nc.scalar.activation(late[:, 1, quarter(q)], plane3[:].indirect(entries(HALF + q * QUARTER, QUARTER)), COPY)
        for q in range(2):
            nc.scalar.copy(out=grouped1[1][:, quarter(q), 2:4], in_=late[:, :, quarter(q)].rearrange("p j s -> p s j"))

        codes1 = keep.tile([P, S], U32, name="codes1", align_bytes=64)
        scales1 = keep.tile([P, S], U8, name="scales1", align_bytes=64)
        for q in range(4):
            quantise(codes1[:, quarter(q)], scales1[:, quarter(q)], grouped1[q // 2][:, quarter(q % 2), :])
        codes = (codes0, codes1)
        planes = {(1, q): scales1[:, quarter(q)] for q in range(4)}
        planes.update({(0, q): scales0[:, quarter(q)] for q in range(3)})
        planes[0, 3] = scales0_last[:]

        duo = psum.tile([N, 2, QUARTER], F32, name="duo")
        solo = psum.tile([N, QUARTER], F32, name="solo")
        trio = {q: psum.tile([N, 3, QUARTER], F32, name="trio%d" % q) for q in range(1, 4)}
        sums = {(m, q): trio[q][:, m, :] for m in range(3) for q in range(1, 4)}
        sums.update({(0, 0): solo[:], (1, 0): duo[:, 0, :], (2, 0): duo[:, 1, :]})

        def one_pass(z, m, q, start, stop):
            nc.tensor.matmul_mx(
                out=sums[m, q],
                lhsT=words[z, m].bitcast(FP8X4),
                lhsT_scale=placed[:, z, m * N : (m + 1) * N],
                rhs=codes[z][:, quarter(q)].bitcast(FP8X4),
                rhs_scale=planes[z, q],
                start=start,
                stop=stop,
            )

        idle = psum.tile([WARM_M, S], F32, name="idle")
        for width in (S, S, QUARTER):
            nc.tensor.matmul_mx(
                out=idle[:, 0:width],
                lhsT=codes0[:, 0:WARM_M].bitcast(FP8X4),
                lhsT_scale=scales0[:, 0:WARM_M],
                rhs=codes0[:, S - width : S].bitcast(FP8X4),
                rhs_scale=wscale[:].rearrange("p z n -> p (z n)")[:, 0:width],
                start=True,
                stop=True,
            )

        for m in range(2):
            for q in range(3):
                one_pass(0, m, q, m == 0 or q == 0, False)
        for q in range(2):
            one_pass(0, 2, q, False, False)
        for q in range(2):
            for m in (1, 2):
                one_pass(1, m, q, False, (m, q) == (2, 0))
        lowest = keep.tile([N, S], F32, name="lowest")
        partial = reuse.tile([N, QUARTER], F32, name="partial", offset=3 * PAIR_BYTES, align_bytes=64)

        def smallest(dst, bank):
            nc.vector.tensor_reduce(out=dst, in_=bank.rearrange("p m s -> p s m"), axis=mybir.AxisListType.X, op=MIN)

        def store(q):
            nc.sync.dma_start(out=out[:, quarter(q)], in_=lowest[:, quarter(q)])

        smallest(partial[:], duo[:])
        one_pass(1, 0, 1, False, True)
        one_pass(1, 0, 0, False, True)
        smallest(lowest[:, quarter(1)], trio[1][:])
        store(1)
        nc.vector.tensor_tensor(lowest[:, quarter(0)], solo[:], partial[:], MIN)
        store(0)
        for q in (2, 3):
            late_passes = [(1, m) for m in range(3)] + [(0, m) for m in range(3) if q == 3 or m == 2]
            for z, m in late_passes:
                one_pass(z, m, q, q == 3 and (z, m) == late_passes[0], (z, m) == late_passes[-1])
            smallest(lowest[:, quarter(q)], trio[q][:])
            store(q)
